import numpy as np, ml_dtypes
CORES = [40,64,80,88,96,104,120,144]
N = 8
BF = ml_dtypes.bfloat16
def gentries(a):
    return np.ascontiguousarray(a.reshape(8, 16, -1).transpose(0, 2, 1)).reshape(8, -1)
def gtable(e):
    e = np.asarray(e); return np.ascontiguousarray(e.reshape(8, -1, 16).transpose(0, 2, 1)).reshape(128, -1).astype(np.int32)
W, C, S, F, HOPS, PH = 4096, 256, 4, 192, 2, 4
R = S * C
def lengths(rng, even):
    return 2 + rng.multinomial(W - F - 2 * C, rng.dirichlet(np.full(C, even)))
def short(rng):
    ln = 2 + (rng.random(C) < 0.3).astype(np.int64); ln[rng.integers(0, C)] += W - F - int(np.sum(ln)); return ln
def near(a, k):
    o, s, at, ln = a
    return o[s + (at + k) % ln]
def away(rng, a):
    return np.roll(near(a, rng.integers(0, W, (S, C))), C // 2, axis=1)
def store(rng, ln, o):
    s = F + np.concatenate([np.zeros(1, np.int64), np.add.accumulate(ln)[:-1]]); who = np.repeat(np.arange(C), ln)
    m = rng.integers(0, W, W); i = np.arange(F, W)
    m[o[F:]] = o[s[who] + (i - s[who] + 1) % ln[who]]
    return m, (o, s, np.minimum((rng.random(C) * ln).astype(np.int64), ln - 1), ln)
def put(o, i, v):
    j = int(np.flatnonzero(o == v)[0]); o[j] = o[i]; o[i] = v
def parts(rng, even=(0.5, 2.0, 20.0), share=0.6, ends=False):
    x = rng.integers(0, 16, (N, 8, 16, W), dtype=np.int32); q = rng.integers(0, 16, (N, 8, 16, R), dtype=np.int32); th = rng.integers(50, 90, (N, 8, R))
    nx = np.zeros((N, 8, W), np.int64); fr = np.zeros((N, 8, F), np.int64); cu = np.zeros((N, 8, C), np.int64); pin = np.zeros((N, 8, R), np.int64); a = {}
    for r in range(N):
        for g in range(8):
            o = rng.permutation(W)
            if ends and g % 4 == 0: put(o, 0, 0); put(o, F - 1, W - 1)
            if ends and g % 4 == 1: put(o, F, 0); put(o, F + 1, W - 1)
            if ends and g % 4 == 2: put(o, 0, W - 1); put(o, W - 1, 0)
            ln = short(rng) if ends else lengths(rng, float(rng.choice(np.array(even))))
            nx[r, g], s = store(rng, ln, o); a[r, g] = s
            fr[r, g] = o[:F]; cu[r, g] = near(s, 0)
            close = rng.random((S, C)) < share * rng.random((1, C))
            pin[r, g] = np.where(close, near(s, rng.integers(-5, 2, (S, C))), rng.integers(0, W, (S, C))).reshape(R)
    return x, nx, fr, cu, q, pin, th, a
def pack(x, nx, fr, cu, q, pin, th):
    return {"x": x.reshape(N, 128, W).astype(np.float32).astype(BF), "nx": nx.astype(np.int32), "fr": fr.astype(np.int32), "cu": np.stack([gtable(v) for v in cu]),
            "q": q.reshape(N, 128, R).astype(np.float32).astype(BF), "pin": np.stack([gtable(v) for v in pin]), "th": np.stack([gtable(v) for v in th])}
def setup_inputs(rng):
    x, nx, fr, cu, q, pin, th, a = parts(rng)
    return pack(x, nx, fr, cu, q, pin, th)
def setup_inputs_alike(rng):
    x, nx, fr, cu, q, pin, th, a = parts(rng)
    for r in range(N):
        for g in range(8):
            s = a[r, g]
            if g % 2 == 0:
                pin[r, g] = rng.choice(np.array([0, W - 1, near(s, 0)[0], near(s, 1)[1]]), R); q[r, g] = q[r, g][:, rng.integers(0, 2, R)]
            else:
                pin[r, g] = np.tile(np.roll(near(s, 0), -1), S); q[r, g] = np.tile(x[r, g][:, np.roll(near(s, 1), -1)], (1, S)); th[:, g] = 0
    return pack(x, nx, fr, cu, q, pin, th)
def setup_inputs_dry(rng):
    x, nx, fr, cu, q, pin, th, a = parts(rng)
    x[:, 4] = rng.integers(0, 16, (N, 16, 1))
    for g in (5, 6):
        x[:, g] = rng.integers(0, 2, (N, 16, 1)); q[:, g] = rng.integers(14, 16, (N, 16, R))
    m = min(C, F); L = F - m; d = C // 8
    for r in range(N):
        for g in range(8):
            s = a[r, g]; p = away(rng, s); T = np.full((S, C), 255); one = near(s, 1)
            if g in (0, 2):
                p = np.array(pin[r, g]).reshape(S, C); p[0] = near(s, 0); p[1] = near(s, 0); T = np.zeros((S, C), np.int64)
                q[r, g, :, :C] = x[r, g][:, one]; q[r, g, :, C:2 * C] = x[r, g][:, near(s, 2)]
            elif g == 4:
                p[0] = near(s, 0); w = rng.permutation(m); u = fr[r, g][rng.permutation(m)]; h = L + m // 2
                nx[r, g, u[:L]] = fr[r, g, m:]; nx[r, g, fr[r, g, m:]] = one[w[:L]]; p[1, w[:L]] = u[:L]; T[1, w[:L]] = 0
                nx[r, g, u[L:h]] = one[w[L:h]]; p[0, w[L:h]] = u[L:h]
            elif g == 5:
                e = m - d; b = L + d; k = int(rng.integers(1, 16)) if r % 2 == 0 else int(rng.integers(16, 48))
                p[0, :e] = near(s, 0)[:e]; T[0, :d] = 0; T[0, d:e] = 80; T[0, b + rng.permutation(e - b)[:k]] = 255
            elif g == 6:
                p[0] = one; T = rng.integers(150, 241, (S, C))
            pin[r, g] = p.reshape(R); th[(r + 1) % N, g] = T.reshape(R)
    return pack(x, nx, fr, cu, q, pin, th)
def setup_inputs_short(rng):
    x, nx, fr, cu, q, pin, th, a = parts(rng, ends=True); th = rng.integers(20, 130, (N, 8, R))
    for r in range(N):
        for g in range(8):
            s = a[r, g]; p = near(s, rng.integers(-2, 2, (S, C))).reshape(R)
            p = np.where(rng.random(R) < 0.25, fr[r, g][rng.integers(0, F, R)], p)
            pin[r, g] = np.where(rng.random(R) < 0.3, rng.integers(0, W, R), p)
            if g < 4: nx[r, g, fr[r, g]] = fr[r, g]
            if g == 7:
                e = np.flatnonzero((s[3] <= HOPS) & (rng.random(C) < 0.5)); v = near(s, 1)[e]; j = (C * np.arange(S)[:, None] + e[None, :]).reshape(-1)
                pin[r, g, j] = np.tile(v, S); q[r, g][:, j] = np.tile(x[r, g][:, v], (1, S)); th[(r + 1) % N, g, j] = 0
    return pack(x, nx, fr, cu, q, pin, th)
def setup_inputs_ties(rng):
    x, nx, fr, cu, q, pin, th, a = parts(rng, share=1.0)
    x[:, ::2] = rng.choice(np.array([2, 5, 6, 9]), (N, 4, 1, W)); q[:, ::2] = rng.integers(1, 11, (N, 4, 1, R)); th[:, ::2] = 16 * rng.integers(0, 5, (N, 4, R))
    x[:, 1::2] = rng.integers(0, 2, (N, 4, 16, W)); q[:, 1::2] = rng.integers(0, 2, (N, 4, 16, R)); th[:, 1::2] = rng.integers(2, 9, (N, 4, R))
    return pack(x, nx, fr, cu, q, pin, th)
def setup_inputs_spread(rng):
    x, nx, fr, cu, q, pin, th, a = parts(rng, even=(0.1, 0.3))
    x = np.minimum((16 * rng.random((N, 8, 16, W)) ** np.exp2(rng.integers(-2, 4, (N, 8, 1, W)))).astype(np.int32), 15)
    q = np.minimum((16 * rng.random((N, 8, 16, R)) ** np.exp2(rng.integers(-2, 4, (N, 8, 1, R)))).astype(np.int32), 15)
    return pack(x, nx, fr, cu, q, pin, rng.integers(0, 160, (N, 8, R)))
def check_inputs(d):
    bad = []
    for k in ("x", "q"):
        v = np.asarray(d[k]).astype(np.float32)
        if not np.all((v >= 0) & (v <= 15) & (v == np.floor(v))): bad.append("whole numbers of " + k)
    for k, hi in (("nx", W - 1), ("fr", W - 1), ("cu", W - 1), ("pin", W - 1), ("th", 255)):
        if np.min(d[k]) < 0 or np.max(d[k]) > hi: bad.append("range of " + k)
    if bad: return bad
    for r in range(N):
        cl = gentries(np.asarray(d["cu"][r])).astype(np.int64)
        for g in range(8):
            f = np.asarray(d["fr"][r][g]).astype(np.int64); m = np.asarray(d["nx"][r][g]).astype(np.int64)
            if len(np.unique(f)) != F:
                bad.append("different numbers of fr"); continue
            live = np.ones(W, bool); live[f] = False; ids = np.flatnonzero(live)
            if not np.array_equal(np.sort(m[ids]), ids) or np.any(m[ids] == ids):
                bad.append("rings of nx"); continue
            jump = np.where(live, m, np.arange(W)); lab = np.arange(W)
            for _ in range(W.bit_length()): lab = np.minimum(lab, lab[jump]); jump = jump[jump]
            if not np.all(live[cl[g]]) or not np.array_equal(np.sort(lab[cl[g]]), np.unique(lab[ids])): bad.append("one cursor in each ring")
    return sorted(set(bad))
def reference(x, nx, fr, cu, q, pin, th):
    X = x.astype(np.float32).astype(np.int32).reshape(N, 8, 16, W); Q = q.astype(np.float32).astype(np.int32).reshape(N, 8, 16, R); M = nx.astype(np.int64)
    c = np.stack([gentries(v) for v in cu]).astype(np.int64); P = np.stack([gentries(v) for v in pin]).astype(np.int64); t = np.stack([gentries(v) for v in th]).astype(np.int64)
    free = {(r, g): fr[r, g].astype(np.int64) for r in range(N) for g in range(8)}
    num = {k: np.zeros(0, np.int64) for k in free}; ring = {k: np.zeros(0, np.int64) for k in free}
    for phase in range(PH):
        n = P; old = P
        for h in range(HOPS):
            n = np.take_along_axis(M, n, 2); xn = np.take_along_axis(X, n[:, :, None, :], 3)
            d = np.add.reduce(np.abs(xn - Q), axis=2)
            if h == 0: least, at, xp = d, n, xn
            else:
                less = d < least
                least = np.where(less, d, least); at = np.where(less, n, at); xp = np.where(less[:, :, None, :], xn, xp)
        P = at; Q = (Q + xp) >> 1
        stay = np.roll(least >= t, -1, axis=0)
        for r, g in free:
            fl = free[r, g]; m = min(C, len(fl)); f = fl[:m]; a = c[r, g, :m].copy(); b = M[r, g, a]
            X[r, g][:, f] = (X[r, g][:, b] + X[r, g][:, a]) >> 1
            M[r, g, f] = M[r, g, b]; M[r, g, a] = f; c[r, g, :m] = f
            v = np.concatenate([num[r, g], b]); w = np.concatenate([ring[r, g], np.arange(m)])
            new4, old4, bit4 = P[r, g].reshape(S, C)[:, w], old[r, g].reshape(S, C)[:, w], stay[r, g].reshape(S, C)[:, w]
            held = np.any((new4 == v) | ((old4 == v) & bit4), axis=0)
            free[r, g] = np.concatenate([fl[m:], v[~held]]); num[r, g] = v[held]; ring[r, g] = w[held]
        if phase < PH - 1: Q = np.roll(Q, 1, axis=0)
    return {"yq": Q.reshape(N, 128, R).astype(np.float32).astype(BF), "yp": np.stack([gtable(v) for v in P]).astype(np.float32), "yn": M.astype(np.float32)}

@@ -1,0 +1,498 @@
+from concourse.mybir import AluOpType, ActivationFunctionType
+
+ALU, AF = AluOpType, ActivationFunctionType
+PH, W, RG = 4, 4096, 192
+NCH, CH = 4, 256
+HALVES, QUARTERS = [(0, 2), (2, 4)], [(0, 1), (1, 2), (2, 3), (3, 4)]
+PRE = [HALVES] * PH
+RD = [HALVES] * PH
+SG = [QUARTERS] * 3 + [HALVES]
+TW = 2 * W + RG
+BF, F32, I32, U16 = "bfloat16", "float32", "int32", "uint16"
+
+
+def sb(n, dtype):
+    return ("sbuf", [128, n], dtype)
+
+
+SCRATCH = {
+    "xt": sb(TW, BF), "mt": sb(TW, BF), "mf": sb(TW, F32), "nxs": sb(256, I32), "hi": sb(256, BF), "lo": sb(256, BF),
+    "ths": sb(64, I32), "cus": sb(16, I32), "frs": sb(RG, I32), "frt": sb(RG, BF), "f0": sb(RG, BF),
+    "qin": sb(4096, BF), "qout": sb(5120, BF), "bin": sb(192, BF), "bout": sb(192, BF),
+    "pu": sb(400, U16), "n1u": sb(320, U16), "n2u": sb(256, U16), "pw": sb(320, I32), "nk": ("sbuf", [128, 4, 2, 80], F32),
+    "g1": sb(4 * 1216, BF), "g2": sb(4 * 1216, BF), "x12": sb(2 * 2240, BF), "ab": ("sbuf", [128, 2, 1024], BF),
+    "ss": sb(1024, BF), "key": sb(128, F32), "km": sb(256, I32), "th8": sb(64, F32),
+    "xab": sb(RG, BF), "xv": sb(3 * RG, BF), "m128": sb(RG, BF), "fu": sb(64, U16), "au": sb(64, U16), "a4": sb(64, F32),
+    "mx": sb(32, F32), "mn": sb(16, I32), "an": sb(16, I32), "valid": sb(36, F32), "v2": sb(36, F32), "retx": sb(144, F32),
+    "eq": sb(4 * 144, BF), "mo": sb(144, BF), "hn": sb(144, BF), "ho": sb(144, BF), "rel": sb(36, BF), "cum": sb(36, BF),
+    "pos": sb(36, F32), "posu": sb(36, U16), "fb": sb(2048 + 3 * RG, BF), "ff": sb(2 * RG, F32),
+    "ci": sb(8, I32), "cf": sb(16, F32), "wi": sb(12, F32), "ioy": sb(144, F32), "iog": sb(128, F32), "iol": sb(16, F32),
+    "iow": sb(3 * RG, BF), "keep": sb(144, BF), "ee": sb(36, F32), "zz": sb(144, BF), "z8": sb(144, BF),
+    "id1": sb(128, BF), "idn": sb(128, BF), "idk": sb(128, BF), "blk": sb(128, BF), "gt0": sb(128, BF), "gtn": sb(128, BF),
+    "l1": sb(10, U16), "l2": sb(4, U16), "ypf": sb(64, F32), "ynf": sb(256, F32),
+}
+SCRATCH.update({b: ("psum", [128, 512], F32) for b in ("d0", "d1", "d2", "d3", "wa", "wb", "wd", "ws")})
+LOADS = ["nx", "xa", "xb", "hi", "lo", "pin", "cu", "th", "fr0", "fr1", "q", "yq0", "yq1", "yp", "yn", "mf"]
+SEMAPHORES = (["dve", "act", "pe", "pool", "sent"] + ["l_" + s for s in LOADS]
+              + ["q%d_%d" % (p, c) for p in range(PH - 1) for c in range(NCH)] + ["b%d" % p for p in range(PH - 1)])
+
+CY, PCY, GA, SC, HOP = 0.00104, 0.00055, 1.55, 3.8, 0.10
+T_Q, T_B, T_CALL = 5.5, 5.0, 0.4
+ALL = slice(None)
+
+
+def A(buf, c0, c1, step=1):
+    return (buf, (ALL, slice(c0, c1, step)), c0, c1, None)
+
+
+def AX(buf, idx, lo, hi, rows=None):
+    return (buf, idx, lo, hi, rows)
+
+
+def width(a):
+    s = a[1][1]
+    return len(range(s.start, s.stop, s.step or 1))
+
+
+def two(*aps):
+    return all(SCRATCH[a[0]][2] in (BF, U16) for a in aps)
+
+
+def build_ops():
+    ops = []
+
+    def add(name, cost, emit, reads, writes, kind="c", lat=0.0, sem=None, after=None):
+        ops.append({"name": name, "cost": cost, "emit": emit, "r": reads, "w": writes, "kind": kind, "lat": lat,
+                    "sem": sem, "after": after})
+        return len(ops) - 1
+
+    def ap(T, a):
+        return T[a[0]][a[1]]
+
+    def ind(T, win, off):
+        return ap(T, win).indirect(ap(T, off))
+
+    def cyc(n):
+        return max(64, n) * CY
+
+    def sc(T, s):
+        return ap(T, s) if isinstance(s, tuple) else s
+
+    def ts(name, out, in0, s1, op0, s2=None, op1=None):
+        n = width(out)
+        cols = [s for s in (s1, s2) if isinstance(s, tuple)]
+
+        def emit(q, T, e, X):
+            if op1 is None:
+                return q.tensor_scalar(ap(T, out), ap(T, in0), sc(T, s1), None, op0)
+            return q.tensor_scalar(ap(T, out), ap(T, in0), sc(T, s1), sc(T, s2), op0, op1)
+        add(name, {"dve": cyc(n / 2 if two(out, in0) else n)}, emit, [in0] + cols, [out])
+
+    def tt(name, out, in0, in1, op):
+        k = 1 if "psum" in (SCRATCH[in0[0]][0], SCRATCH[in1[0]][0]) else 2
+        add(name, {"dve": cyc(k * width(out))}, lambda q, T, e, X: q.tensor_tensor(ap(T, out), ap(T, in0), ap(T, in1), op),
+            [in0, in1], [out])
+
+    def cp(name, out, in_):
+        n = width(out)
+        add(name, {"dve": cyc(n / 2 if two(out, in_) else n)}, lambda q, T, e, X: q.tensor_copy(ap(T, out), ap(T, in_)),
+            [in_], [out])
+
+    def lin(name, out, in_, scale, bias):
+        n = width(in_)
+
+        def emit(q, T, e, X):
+            if e == "act":
+                if bias == 0.0:
+                    return q.activation(ap(T, out), ap(T, in_), AF.Copy, scale=scale)
+                return q.activation(ap(T, out), ap(T, in_), AF.Identity, bias=bias, scale=scale)
+            return q.tensor_scalar(ap(T, out), ap(T, in_), scale, bias, ALU.mult, ALU.add)
+        add(name, {"act": cyc(n), "dve": cyc(n / 2 if two(out, in_) else n)}, emit, [in_], [out])
+
+    def gather(name, out, win, off):
+        n = 16 * width(off)
+
+        def emit(q, T, e, X):
+            if e == "act":
+                return q.activation(ap(T, out), ind(T, win, off), AF.Copy)
+            return q.tensor_copy(ap(T, out), ind(T, win, off))
+        add(name, {"act": 0.065 + GA * n * CY, "dve": 0.05 + GA * n * CY}, emit, [win, off], [out])
+
+    def gtt(name, out, win, off, in1, op):
+        add(name, {"dve": 0.05 + GA * 16 * width(off) * CY},
+            lambda q, T, e, X: q.tensor_tensor(ap(T, out), ind(T, win, off), ap(T, in1), op), [win, off, in1], [out])
+
+    def scatter(name, win, off, in_, in1=None):
+        def emit(q, T, e, X):
+            if in1 is None:
+                return q.tensor_copy(ind(T, win, off), ap(T, in_))
+            return q.tensor_tensor(ind(T, win, off), ap(T, in_), ap(T, in1), ALU.add)
+        add(name, {"dve": 0.05 + SC * 16 * width(off) * CY}, emit, [off, in_] + ([in1] if in1 else []), [win])
+
+    def scan(name, out, d0, d1, op0, op1):
+        add(name, {"dve": cyc(width(out) / 2)},
+            lambda q, T, e, X: q.tensor_tensor_scan(ap(T, out), ap(T, d0), ap(T, d1), 0.0, op0, op1), [d0, d1], [out])
+
+    def mm(name, parts, first=True, last=True):
+        def emit(q, T, e, X):
+            ins = None
+            for k, (o, l, r) in enumerate(parts):
+                ins = q.matmul(ap(T, o), ap(T, l), ap(T, r), first and k == 0, last and k == len(parts) - 1)
+            return ins
+        add(name, {"pe": sum(max(64, width(o)) for o, l, r in parts) * PCY}, emit,
+            [x for o, l, r in parts for x in (l, r)], [o for o, l, r in parts])
+
+    def wrap(name, bank, buf, c0, c1):
+        mm(name, [(A(bank, 0, (c1 - c0) // 16), A("zz", 15 - i, 143 - i), A(buf, c0 + i, c1, 16)) for i in range(16)])
+
+    def memset(name, out, v):
+        add(name, {"dve": cyc(width(out) / 2 if two(out) else width(out))}, lambda q, T, e, X: q.memset(ap(T, out), v), [], [out])
+
+    def iota(name, out, pat, base, cm):
+        def emit(q, T, e, X):
+            if SCRATCH[out[0]][2] == I32:
+                return q.iota(ap(T, out), pat, base, cm)
+            return q.iota(ap(T, out), pat, base, cm, allow_small_or_imprecise_dtypes=True)
+        add(name, {"pool": 0.16 + 2 * width(out) * CY}, emit, [], [out])
+
+    def load(sem, eng, out, src, lat, behind=()):
+        add("l_" + sem, {eng: 0.06}, lambda q, T, e, X: q.dma_start(ap(T, out), src(T)), list(behind), [out], "dma", lat, "l_" + sem)
+
+    def move(sem, eng, out, in_, lat):
+        add("l_" + sem, {eng: 0.06}, lambda q, T, e, X: q.dma_start(ap(T, out), ap(T, in_)), [in_], [out], "dma", lat, "l_" + sem)
+
+    def store(sem, eng, dst, in_, lat):
+        add("l_" + sem, {eng: 0.06}, lambda q, T, e, X: q.dma_start(dst(T), ap(T, in_)), [in_], [], "dma", lat, "l_" + sem)
+
+    def send(sem, way, out, in_, lat):
+        def emit(q, T, e, X):
+            rid, pid, mask = X[way]
+            q.remote_dma(ap(T, out), ap(T, in_), T.sem[sem], T.sem.sent, pid, rid, mask)
+        k = add("s_" + sem, {"pool": T_CALL}, emit, [in_], [], "send")
+        add("r_" + sem, {}, way, [], [out], "recv", lat, sem, k)
+
+    def rows(buf, r, c1):
+        return AX(buf, (slice(r, 128, 16), slice(0, c1)), 0, c1, r)
+
+    def col(buf, k):
+        return A(buf, k, k + 1)
+
+    def nk(p, hop, k0, k1):
+        return AX("nk", (ALL, p, hop, slice(k0, k1)), 160 * p + 80 * hop + k0, 160 * p + 80 * hop + k1)
+
+    xw, mw = A("xt", 0, W), A("mt", 0, W)
+    id1, idn, blk = A("id1", 0, 128), A("idn", 0, 128), A("blk", 0, 128)
+    load("nx", "sp", A("nxs", 0, 256), lambda T: T.nx[:], 2.2)
+    load("pin", "act", A("pw", 0, 64), lambda T: T.pin[:], 2.2)
+    load("xa", "sp", A("xt", 0, W // 2), lambda T: T.x[:, 0:W // 2], 3.8)
+    load("cu", "act", A("cus", 0, 16), lambda T: T.cu[:], 2.2)
+    memset("z_mt", A("mt", 0, W // 2), 0.0)
+    lin("z_mt2", A("mt", W // 2, W), A("mt", 0, W // 2), 1.0, 0.0)
+    cp("hi", A("hi", 0, 256), A("nxs", 0, 256))
+    tt("lo", A("lo", 0, 256), A("nxs", 0, 256), A("hi", 0, 256), ALU.subtract)
+    move("hi", "sp", rows("mt", 0, W), A("hi", 0, 256), 2.2)
+    move("lo", "sp", rows("mt", 1, W), A("lo", 0, 256), 2.2)
+    load("xb", "sp", A("xt", W // 2, W), lambda T: T.x[:, W // 2:W], 3.6, [A("hi", 0, 256)])
+    load("q", "sp", A("qin", 0, 1024), lambda T: T.q[:], 3.6, [A("lo", 0, 256)])
+    load("th", "sp", A("ths", 0, 64), lambda T: T.th[:], 2.2)
+    memset("z_fr", A("frs", 0, RG), 0)
+    load("fr0", "sp", rows("frs", 0, RG), lambda T: T.fr[:], 2.2)
+    load("fr1", "sp", rows("frs", 1, RG), lambda T: T.fr[:], 2.2)
+    iota("i_p", col("ci", 0), [[0, 1]], 0, 1)
+    iota("i_pf", col("cf", 0), [[0, 1]], 0, 1)
+    iota("i_y", A("ioy", 0, 144), [[1, 144]], 0, 0)
+    iota("i_l", A("iol", 0, 9), [[0, 3], [4, 3]], 0, 0)
+    iota("i_g", A("iog", 0, 128), [[1, 8], [0, 16]], 0, 0)
+    iota("i_w", A("iow", 0, 3 * RG), [[0, 3], [1, RG]], 0, 0)
+    iota("i_k", A("keep", 0, 144), [[0, 36], [1, 4]], 0, 0)
+    iota("i_e", A("ee", 0, 36), [[16, 36]], 257, 1)
+    ts("c_g", col("ci", 1), col("ci", 0), 4, ALU.logical_shift_right)
+    ts("c_zc", col("cf", 1), col("ci", 1), 16.0, ALU.mult, 15.0, ALU.add)
+    ts("c_z", A("zz", 0, 144), A("ioy", 0, 144), col("cf", 1), ALU.is_equal)
+    lin("c_z8", A("z8", 0, 144), A("zz", 0, 144), 8192.0, 0.0)
+    ts("c_b", col("ci", 2), col("ci", 0), 3, ALU.bitwise_and)
+    ts("c_a", col("ci", 3), col("ci", 0), 2, ALU.logical_shift_right, 3, ALU.bitwise_and)
+    cp("c_af", col("cf", 3), col("ci", 3))
+    ts("c_h", col("cf", 5), col("ci", 2), 16.0, ALU.mult, col("cf", 3), ALU.add)
+    ts("c_l1", A("l1", 0, 9), A("iol", 0, 9), col("cf", 5), ALU.add)
+    ts("c_l2", A("l2", 0, 3), A("iol", 0, 3), col("cf", 3), ALU.add)
+    ts("c_i", col("ci", 4), col("ci", 0), 15, ALU.bitwise_and)
+    ts("c_m1", col("cf", 6), col("ci", 4), 1.0, ALU.is_equal)
+    ts("c_m0", col("cf", 7), col("ci", 4), 0.0, ALU.is_equal, 2.0 * W, ALU.mult)
+    cp("c_if", col("cf", 9), col("ci", 4))
+    ts("c_wi", A("wi", 0, 12), A("ioy", 0, 12), 16.0, ALU.mult, col("cf", 9), ALU.add)
+    cp("c_gf", col("cf", 8), col("ci", 1))
+    ts("c_id", id1, A("ioy", 0, 128), col("cf", 0), ALU.is_equal)
+    lin("c_idn", idn, id1, -1.0, 0.0)
+    lin("c_idk", A("idk", 0, 128), id1, 2048.0, 0.0)
+    ts("c_blk", blk, A("iog", 0, 128), col("cf", 8), ALU.is_equal)
+    ts("c_gt0", A("gt0", 0, 128), A("ioy", 0, 128), col("cf", 0), ALU.is_lt, -1.0, ALU.mult)
+    tt("c_gtn", A("gtn", 0, 128), A("gt0", 0, 128), blk, ALU.mult)
+    ts("c_fb", A("fb", 2048, 2048 + 3 * RG), A("iow", 0, 3 * RG), col("cf", 6), ALU.mult, col("cf", 7), ALU.add)
+    memset("c_m128", A("m128", 0, RG), -128.0)
+    cp("pinu", A("pu", 0, 64), A("pw", 0, 64))
+    cp("cuu", A("pu", 64, 76), A("cus", 0, 12))
+    ts("cu4", A("a4", 0, 12), A("cus", 0, 12), float(W), ALU.add)
+    ts("th8", A("th8", 0, 64), A("ths", 0, 64), 8192.0, ALU.mult)
+    ts("fr_t", A("frt", 0, RG), A("frs", 0, RG), col("cf", 6), ALU.mult)
+    tt("fr_d", A("f0", 0, RG), A("frs", 0, RG), A("frt", 0, RG), ALU.subtract)
+
+    for p in range(PH):
+        last = p == PH - 1
+        fbuf, fc = ("f0", 0) if p == 0 else ("fb", 2048 + RG * (p - 1))
+        U, G, K, XC = 80 * p, 1216 * p, p + 1, 2240 * (p % 2)
+        fu, au, a4 = A("fu", 16 * p, 16 * p + 12), A("au", 16 * p, 16 * p + 12), A("a4", 16 * p, 16 * p + 12)
+        if p == 0:
+            au = A("pu", 64, 76)
+        fw = A("ws", 0, 12)
+        wrap("wf%d" % p, "ws", fbuf, fc, fc + RG)
+        cp("fu%d" % p, fu, fw)
+        if not last:
+            tt("mn%d" % p, A("mn", 0, 12), fw, a4, ALU.min)
+            ts("va%d" % p, A("valid", 12 * p, 12 * p + 12), fw, float(W), ALU.is_lt)
+            ts("an%d" % p, A("an", 0, 12), A("mn", 0, 12), W - 1, ALU.bitwise_and)
+            cp("anu%d" % p, A("pu", U + 144, U + 156), A("an", 0, 12))
+            ts("a4%d" % p, A("a4", 16 * p + 16, 16 * p + 28), A("an", 0, 12), float(W), ALU.add)
+        for h, (ca, cb) in enumerate(PRE[p]):
+            k0, k1 = 16 * ca, 16 * cb
+            ke = k1 + (12 if cb == NCH else 0)
+            bank = "wa" if h % 2 == 0 else "wb"
+            nm = "%d_%d" % (p, h)
+            gather("g1_" + nm, A("g1", G + 16 * k0, G + 16 * ke), mw, A("pu", U + k0, U + ke))
+            wrap("w1_" + nm, bank, "g1", G + 16 * k0, G + 16 * ke)
+            cp("n1u_" + nm, A("n1u", U + k0, U + ke), A(bank, 0, ke - k0))
+            lin("nk1_" + nm, nk(p, 0, k0, ke), A(bank, 0, ke - k0), 1.0, 0.0)
+            gather("g2_" + nm, A("g2", G + 16 * k0, G + 16 * ke), mw, A("n1u", U + k0, U + ke))
+            wrap("w2_" + nm, bank, "g2", G + 16 * k0, G + 16 * k1)
+            cp("n2u_" + nm, A("n2u", 64 * p + k0, 64 * p + k1), A(bank, 0, k1 - k0))
+            lin("nk2_" + nm, nk(p, 1, k0, k1), A(bank, 0, k1 - k0), 1.0, float(W))
+            kx = k1 if last else ke
+            gather("x1_" + nm, A("x12", XC + 16 * k0, XC + 16 * kx), xw, A("n1u", U + k0, U + kx))
+            gather("x2_" + nm, A("x12", XC + 1216 + 16 * k0, XC + 1216 + 16 * k1), xw, A("n2u", 64 * p + k0, 64 * p + k1))
+        if not last:
+            gather("xa%d" % p, A("xab", 0, RG), xw, A("pu", U + 64, U + 76))
+            mm("xs%d" % p, [(A("ws", 0, RG), id1, A("xab", 0, RG)), (A("ws", 0, RG), id1, A("x12", XC + 1024, XC + 1216))])
+            lin("xv%d" % p, A("xv", RG * p, RG * p + RG), A("ws", 0, RG), 0.5, 127.75)
+            scatter("sa%d" % p, A("mt", 0, TW), au, A(fbuf, fc, fc + RG))
+            scatter("sf%d" % p, A("mt", 0, TW), fu, A("g2", G + 1024, G + 1216))
+        else:
+            mm("wn", [(A("wa", 0, 256), A("zz", 15 - i, 143 - i), A("mt", 256 * i, 256 * i + 256)) for i in range(16)])
+            lin("ynf", A("ynf", 0, 256), A("wa", 0, 256), 1.0, 0.0)
+            move("mf", "sp", rows("mf", 0, W), A("ynf", 0, 256), 2.6)
+            mm("nbs", [(A("wb", 0, RG), blk, A("g2", G + 1024, G + 1216))])
+            lin("nbf", A("ff", RG, 2 * RG), A("wb", 0, RG), 1.0, 0.0)
+            mm("fs", [(A("wb", 0, RG), blk, A(fbuf, fc, fc + RG))])
+            lin("ff", A("ff", 0, RG), A("wb", 0, RG), 1.0, 0.0)
+            scatter("sa%d" % p, A("mf", 0, TW), au, A("ff", 0, RG))
+            scatter("sf%d" % p, A("mf", 0, TW), fu, A("ff", RG, 2 * RG))
+        for h, (ca, cb) in enumerate(RD[p]):
+            for c in range(ca, cb):
+                nm = "%d_%d" % (p, c)
+                bank, xc, qa = "d%d" % c, XC + CH * c, A("qin", 1024 * p + CH * c, 1024 * p + CH * c + CH)
+                mm("dx" + nm, [(A(bank, 0, CH), id1, A("x12", xc, xc + CH)),
+                               (A(bank, CH, 2 * CH), id1, A("x12", xc + 1216, xc + 1216 + CH))], True, False)
+                mm("dq" + nm, [(A(bank, 0, CH), idn, qa), (A(bank, CH, 2 * CH), idn, qa)], False, True)
+                ab = AX("ab", (ALL, ALL, slice(CH * c, CH * c + CH)), CH * c, CH * c + CH)
+                add("abs" + nm, {"act": cyc(512)},
+                    lambda q, T, e, X, ab=ab, bank=bank, p=p: q.activation(ap(T, ab), T[bank][:, 0:512], AF.Abs, bias=128.0 if p else 0.0),
+                    [A(bank, 0, 512)], [ab])
+            nm, k0, k1, n = "%d_%d" % (p, h), 16 * ca, 16 * cb, 16 * (cb - ca)
+            mm("wd" + nm, [(A("wd", 0, 2 * n), A("z8", 15 - i, 143 - i),
+                            AX("ab", (ALL, ALL, slice(CH * ca + i, CH * cb, 16)), CH * ca, CH * cb)) for i in range(16)])
+            tt("key" + nm, A("key", 2 * k0, 2 * k1), A("wd", 0, 2 * n),
+               AX("nk", (ALL, p, ALL, slice(k0, k1)), 160 * p + k0, 160 * p + 80 + k1), ALU.add)
+            km = A("km", 64 * p + k0, 64 * p + k1)
+            tt("min" + nm, km, A("key", 2 * k0, 2 * k0 + n), A("key", 2 * k0 + n, 2 * k1), ALU.min)
+            ts("and" + nm, A("pw", 64 * p + 64 + k0, 64 * p + 64 + k1), km, W - 1, ALU.bitwise_and)
+            cp("pu" + nm, A("pu", U + 80 + k0, U + 80 + k1), A("pw", 64 * p + 64 + k0, 64 * p + 64 + k1))
+            if cb == NCH and not last:
+                tt("bit%d" % p, A("bout", 64 * p, 64 * p + 64), A("km", 64 * p, 64 * p + 64), A("th8", 0, 64), ALU.is_ge)
+                send("b%d" % p, "b", A("bin", 64 * p, 64 * p + 64), A("bout", 64 * p, 64 * p + 64), T_B)
+            for sa, sz in SG[p]:
+                if not ca <= sa < cb:
+                    continue
+                nm, q0, q1 = "%d_%d" % (p, sa), 1024 * p + CH * sa, 1024 * p + CH * sz
+                ss = A("ss", CH * sa, CH * sz)
+                gtt("sg" + nm, ss, xw, A("pu", U + 80 + 16 * sa, U + 80 + 16 * sz), A("qin", q0, q1), ALU.add)
+                lin("half" + nm, A("qout", q0, q1), ss, 0.5, 63.75 if p else 127.75)
+                if last:
+                    lin("fin" + nm, A("qout", q0 + 1024, q1 + 1024), A("qout", q0, q1), 1.0, -128.0)
+                    continue
+                for c in range(sa, sz):
+                    qc = 1024 * p + CH * c
+                    send("q%d_%d" % (p, c), c, A("qin", qc + 1024, qc + 1024 + CH), A("qout", qc, qc + CH), T_Q)
+        if last:
+            break
+        scatter("sx%d" % p, A("xt", 0, TW), fu, A("xv", RG * p, RG * p + RG), A("m128", 0, RG))
+        n4, n1 = 48 * K, 12 * K
+        gather("rx%d" % p, A("retx", 48 * p, n4), nk(p, 0, 64, 76), A("l2", 0, 3))
+        l1 = A("l1", 0, 3 * K)
+        eqo, eqn = A("eq", 144 * p, 144 * p + n4), A("eq", 144 * K, 144 * K + n4)
+        gtt("eqo%d" % p, A("eq", 192 * p, 192 * p + 48), A("pw", 64 * p, 64 * p + 64), A("l1", 0, 3), A("retx", 48 * p, n4), ALU.is_equal)
+        gtt("eqn%d" % p, eqn, A("pw", 64 * p + 64, 64 * p + 128), l1, A("retx", 0, n4), ALU.is_equal)
+        scan("hn%d" % p, A("hn", 0, n4), A("keep", 0, n4), eqn, ALU.mult, ALU.max)
+        tt("v2%d" % p, A("v2", 0, n1), A("valid", 0, n1), A("hn", 3, n4, 4), ALU.is_gt)
+        gtt("mo%d" % p, A("mo", 0, n4), A("bin", 64 * p, 64 * p + 64), l1, eqo, ALU.mult)
+        scan("ho%d" % p, A("ho", 0, n4), A("keep", 0, n4), A("mo", 0, n4), ALU.mult, ALU.max)
+        rel, cum = A("rel", 0, n1), A("cum", 0, n1)
+        tt("rel%d" % p, rel, A("v2", 0, n1), A("ho", 3, n4, 4), ALU.is_gt)
+        scan("cum%d" % p, cum, rel, rel, ALU.add, ALU.max)
+        mm("rk%d" % p, [(A("ws", 0, n1), A("gtn", 0, 128), rel), (A("ws", 0, n1), A("idk", 0, 128), rel),
+                        (A("ws", 0, n1), blk, cum), (A("ws", 40, 41), blk, A("cum", n1 - 1, n1))])
+        tt("pos%d" % p, A("pos", 0, n1), A("ws", 0, n1), A("ee", 0, n1), ALU.max)
+        ts("posu%d" % p, A("posu", 0, n1), A("pos", 0, n1), -1.0, ALU.add)
+        ts("ac%d" % p, A("mx", 0, 12), A("wi", 0, 12), A("ws", 40, 41), ALU.is_lt, -float(W), ALU.mult)
+        tt("ad%d" % p, A("mx", 16, 28), A("mx", 0, 12), A("a4", 16 * p + 16, 16 * p + 28), ALU.add)
+        cp("au%d" % p, A("au", 16 * p + 16, 16 * p + 28), A("mx", 16, 28))
+        if p < PH - 2:
+            tt("vv%d" % p, A("valid", 0, n1), A("valid", 0, n1), rel, ALU.subtract)
+        for k in range(K):
+            scatter("sl%d_%d" % (p, k), A("fb", RG * p, RG * p + 2048 + RG), A("posu", 12 * k, 12 * k + 12),
+                    A("g1", 1216 * k + 1024, 1216 * k + 1216))
+    store("yq0", "sp", lambda T: T.yq[:, 0:512], A("qout", 4096, 4608), 2.6)
+    store("yq1", "sp", lambda T: T.yq[:, 512:1024], A("qout", 4608, 5120), 2.6)
+    cp("ypf", A("ypf", 0, 64), A("pw", 256, 320))
+    store("yp", "sp", lambda T: T.yp[:], A("ypf", 0, 64), 2.2)
+    store("yn", "sp", lambda T: T.yn[:], rows("mf", 0, W), 2.6)
+    return ops
+
+
+def meet(a, b):
+    if a[0] != b[0]:
+        return False
+    if SCRATCH[a[0]][0] == "psum":
+        return True
+    return a[2] < b[3] and b[2] < a[3] and (a[4] is None or b[4] is None or a[4] == b[4])
+
+
+def find_deps(ops):
+    deps = []
+    for k, o in enumerate(ops):
+        d = {}
+        for j in range(k):
+            e = ops[j]
+            if any(meet(a, b) for a in o["r"] + o["w"] for b in e["w"]) or any(meet(a, b) for a in o["w"] for b in e["r"]):
+                d[j] = False
+            elif any(SCRATCH[a[0]][0] == "psum" and meet(a, b) for a in o["r"] for b in e["r"]):
+                d[j] = True
+        if o["after"] is not None:
+            d[o["after"]] = False
+        deps.append(d)
+    return deps
+
+
+ORDER = """
+17 16 21 0 4 13 2 5 12 1a 6 7 20 24 25 51 3a 34 48 14 15 35 52 19 8 53 39 18 26 50 9 10 27 54 40 41 49 71a 61 62 37 72 63 55 65a
+64 73 75 74a 66 67 69a 22 70a 23 42 11 28 76 77 79 80a 89 90 84 91a 86 87 88a 78a 56 105 108 68a 106 107a 81a 85 92 93 29 94 95
+96 97 109 110a 101 111 98 112 57 113 58 114 59 115 116 123 47 152a 153 124 30 119 99 154 31 120 33 43 102a 82 162a 163 44 128 32
+45 83a 164 165 155a 156a 157 127 166a 130 158 161a 129 160 167 131 168 170 103 117 118 177 180 104 133 132 134 125 100 178 38 135
+121 36 171a 181 136 199 46 137 138 60 169a 140 139 141 196 144 179a 182a 126 142 159a 122 200 201a 183 184 197 175 145 185 146
+147 198a 202 176 203 186 204 187 207 205 149 188 148 150 206 192 210 193 172a 173 214 211 244a 245 246 189a 174a 218 215 254a 255
+247 256 248a 219 208 221 258 143 249 222 257 250 252a 190 194 220 223 212 262a 191 259 253a 209 224 225 226 227 216 228 260 263a
+269 272 264a 270 271a 151 213 195 291 273 229 231 274a 230 232 288 235 233 311a 261a 217 289 290a 236 267 237 238 292 239 268
+251a 275 276 241 293a 294 277 278 279 240 295 296 297 299 284 300 331a 332 285a 280 298 242 281a 286 333 335a 302 341 306 334a
+265 336 337 307 338 342 234 343 313 303a 266a 310 345a 282 287 312 349 301 314 304 316 344a 340a 315 317 318 319 351 339a 346
+352a 305 347 348 320 321 363 323 322 243 350a 326 327 324 364 365a 283 360 361 377 362a 374 308 375 366 328 367 325 368 369 370
+376a 309 378 379a 354 355a 371 380 381 329 356 372a 353 357a 373a 382 383 384 385 388 330 358 359 386a 387a 389 392 390 391
+"""
+
+
+def plan():
+    ops = build_ops()
+    deps = find_deps(ops)
+    order, eng = [], [None] * len(ops)
+    for word in ORDER.split():
+        k = int(word.rstrip("a"))
+        able = list(ops[k]["cost"]) or [None]
+        eng[k] = able[0] if len(able) == 1 else ("act" if word.endswith("a") else "dve")
+        assert all(j in order for j in deps[k])
+        order.append(k)
+    assert len(set(order)) == len(ops)
+    return ops, deps, eng, order
+
+
+PLAN = []
+
+
+def ways(T, topo, r):
+    src, out = T.cores[r], {}
+    for names, dst in ((list(range(NCH)), T.cores[(r + 1) % len(T.cores)]), (["b"], T.cores[r - 1])):
+        if topo.may_write(src, dst):
+            for s in names:
+                out[s] = [src, dst]
+            continue
+        able = [c for c in topo.cores_of(src) if T.rank_of(c) is None and topo.may_write(c, dst)]
+        near = [c for c in able if topo.die(c) == topo.die(src)]
+        far = [c for c in able if c not in near]
+        turn = [c for pair in zip(near, far) for c in pair] or able
+        for k, s in enumerate(names):
+            out[s] = [src, turn[k % len(turn)], dst]
+    return out
+
+
+def relay_program(g, core, T, topo, ops, order):
+    sent = 0
+    for r in [r for r, c in enumerate(T.cores) if core in topo.cores_of(c)]:
+        way = ways(T, topo, r)
+        for k in order:
+            if ops[k]["kind"] != "send":
+                continue
+            o = ops[k + 1]
+            if len(way[o["emit"]]) == 3 and way[o["emit"]][1] == core:
+                src, me, dst = way[o["emit"]]
+                piece = T[o["w"][0][0]][o["w"][0][1]]
+                rid, pid = topo.addr(dst, core)
+                g.wait_ge(T.sem[o["sem"]], len(topo.engines(src, core)))
+                g.remote_dma(piece, piece, T.sem[o["sem"]], T.sem.sent, pid, rid, topo.mask(core, dst))
+                sent += len(topo.engines(core, dst))
+    if sent:
+        g.wait_ge(T.sem.sent, sent)
+
+
+def rank_program(g, core, T, topo):
+    if not PLAN:
+        PLAN.append(plan())
+    ops, deps, eng, order = PLAN[0]
+    rank = T.rank_of(core)
+    if rank is None:
+        relay_program(g, core, T, topo, ops, order)
+        return
+    n = len(T.cores)
+    out = ways(T, topo, rank)
+    X = {s: topo.addr(w[1], core) + (topo.mask(core, w[1]),) for s, w in out.items()}
+    comes = dict(ways(T, topo, (rank - 1) % n))
+    comes["b"] = ways(T, topo, (rank + 1) % n)["b"]
+    token, total, sent = {}, {}, 0
+    for k in order:
+        o = ops[k]
+        if o["kind"] == "c":
+            total[eng[k]] = total.get(eng[k], 0) + 1
+            token[k] = (eng[k], total[eng[k]])
+        elif o["kind"] == "dma":
+            token[k] = (o["sem"], 16)
+        elif o["kind"] == "recv":
+            token[k] = (o["sem"], len(topo.engines(comes[o["emit"]][-2], core)))
+            sent += len(topo.engines(core, out[o["emit"]][1]))
+    queue = {"dve": g.vector, "act": g.scalar, "pe": g.tensor, "pool": g, "sp": g.sync}
+    waited, seen = {}, {e: {} for e in queue}
+    for k in order:
+        e = eng[k]
+        if e is None:
+            continue
+        need = {}
+        for j, both_read in deps[k].items():
+            if not (eng[j] == e and (e == "pe" or both_read)):
+                s, v = token[j]
+                need[s] = max(need.get(s, 0), v)
+        for s, v in need.items():
+            if seen[e].get(s, 0) < v:
+                queue[e].wait_ge(T.sem[s], v)
+                seen[e][s] = v
+                waited[s] = max(waited.get(s, 0), v)
+        ins = ops[k]["emit"](queue[e], T, e, X)
+        if ops[k]["kind"] != "send":
+            ins.then_inc(T.sem[token[k][0]], 1 if ops[k]["kind"] == "c" else 16)
+    g.wait_ge(T.sem.sent, sent)
+    for s, v in list(total.items()) + [t for k, t in token.items() if ops[k]["kind"] != "c"]:
+        if waited.get(s, 0) < v:
+            g.sync.wait_ge(T.sem[s], v)

@@ -2,56 +2,69 @@ from concourse.mybir import AluOpType, ActivationFunctionType
 
 ALU, AF = AluOpType, ActivationFunctionType
 PH, W, RG = 4, 4096, 192
-NCH, CH = 4, 256
-HALVES, QUARTERS = [(0, 2), (2, 4)], [(0, 1), (1, 2), (2, 3), (3, 4)]
-PRE = [HALVES] * PH
-RD = [HALVES] * PH
-SG = [QUARTERS] * 3 + [HALVES]
+NCH, CH, HF = 4, 256, 512
 TW = 2 * W + RG
 BF, F32, I32, U16 = "bfloat16", "float32", "int32", "uint16"
+SCL = [2.0 ** (p - 4) for p in range(PH)]
+QB = [241.0, 177.0, 145.0, 129.0]
+TB = [113.0, 113.0, 113.0, -127.0]
+MODE = ["hop", "chunk", "chunk", "chunk"]
+LAST = [1, 1]
+SILU = [False, False, False]
+RND = 1.5 * 2 ** 23
 
 
 def sb(n, dtype):
-    return ("sbuf", [128, n], dtype)
+    return ("sbuf", [128] + (n if isinstance(n, list) else [n]), dtype)
 
 
 SCRATCH = {
-    "xt": sb(TW, BF), "mt": sb(TW, BF), "mf": sb(TW, F32), "nxs": sb(256, I32), "hi": sb(256, BF), "lo": sb(256, BF),
+    "xt": sb(TW, BF), "mt": sb(TW, BF), "mf": sb(TW, F32), "nxs": sb(256, I32), "dg": sb(512, BF), "qraw": sb(1024, BF),
     "ths": sb(64, I32), "cus": sb(16, I32), "frs": sb(RG, I32), "frt": sb(RG, BF), "f0": sb(RG, BF),
-    "qin": sb(4096, BF), "qout": sb(5120, BF), "bin": sb(192, BF), "bout": sb(192, BF),
-    "pu": sb(400, U16), "n1u": sb(320, U16), "n2u": sb(256, U16), "pw": sb(320, I32), "nk": ("sbuf", [128, 4, 2, 80], F32),
-    "g1": sb(4 * 1216, BF), "g2": sb(4 * 1216, BF), "x12": sb(2 * 2240, BF), "ab": ("sbuf", [128, 2, 1024], BF),
-    "ss": sb(1024, BF), "key": sb(128, F32), "km": sb(256, I32), "th8": sb(64, F32),
-    "xab": sb(RG, BF), "xv": sb(3 * RG, BF), "m128": sb(RG, BF), "fu": sb(64, U16), "au": sb(64, U16), "a4": sb(64, F32),
-    "mx": sb(32, F32), "mn": sb(16, I32), "an": sb(16, I32), "valid": sb(36, F32), "v2": sb(36, F32), "retx": sb(144, F32),
-    "eq": sb(4 * 144, BF), "mo": sb(144, BF), "hn": sb(144, BF), "ho": sb(144, BF), "rel": sb(36, BF), "cum": sb(36, BF),
+    "qin": sb(4096, BF), "qout": sb(4096, BF), "bin": sb(192, BF), "kin": sb(192, I32), "thn": sb(64, F32),
+    "pu": sb([10, 80], U16), "pw": sb([10, 64], I32), "km": sb([8, 64], I32), "key": sb([4, 2, 32], F32),
+    "n1u": sb(320, U16), "n2u": sb(256, U16), "nk": sb([4, 2, 80], F32), "jc": sb(64, F32),
+    "g0": sb(4 * 1216, BF), "g1": sb(1216, BF), "xh": sb(8 * HF, BF), "ab": sb([2, 1024], BF), "ss": sb(1024, BF),
+    "th8": sb(64, F32), "xab": sb(2 * RG, BF), "xv": sb(RG, BF), "m128": sb(RG, BF),
+    "fu": sb(64, U16), "au": sb(64, U16), "a4": sb(64, F32), "mx": sb(16, F32), "mn": sb(16, F32), "valid": sb(48, F32),
+    "retx": sb(144, F32), "hm": sb(4 * 288, BF), "ho": sb(288, BF), "rel": sb(36, BF), "cum": sb(36, BF),
     "pos": sb(36, F32), "posu": sb(36, U16), "fb": sb(2048 + 3 * RG, BF), "ff": sb(2 * RG, F32),
+    "fw": sb(2048 + 3 * RG, F32), "fs": sb(3 * RG, F32),
     "ci": sb(8, I32), "cf": sb(16, F32), "wi": sb(12, F32), "ioy": sb(144, F32), "iog": sb(128, F32), "iol": sb(16, F32),
-    "iow": sb(3 * RG, BF), "keep": sb(144, BF), "ee": sb(36, F32), "zz": sb(144, BF), "z8": sb(144, BF),
-    "id1": sb(128, BF), "idn": sb(128, BF), "idk": sb(128, BF), "blk": sb(128, BF), "gt0": sb(128, BF), "gtn": sb(128, BF),
+    "ioj": sb(64, F32), "iow": sb(3 * RG, BF), "keep": sb(288, BF), "ee": sb(36, F32),
+    "zz": sb(144, BF), "z8": sb(144, BF), "zf": sb(144, BF), "id1": sb(128, BF), "idn": sb(128, BF), "idk": sb(128, BF),
+    "blk": sb(128, BF), "gt0": sb(128, BF), "gtn": sb(128, BF), "apart": sb(144, F32),
     "l1": sb(10, U16), "l2": sb(4, U16), "ypf": sb(64, F32), "ynf": sb(256, F32),
 }
-SCRATCH.update({b: ("psum", [128, 512], F32) for b in ("d0", "d1", "d2", "d3", "wa", "wb", "wd", "ws")})
-LOADS = ["nx", "xa", "xb", "hi", "lo", "pin", "cu", "th", "fr0", "fr1", "q", "yq0", "yq1", "yp", "yn", "mf"]
-SEMAPHORES = (["dve", "act", "pe", "pool", "sent"] + ["l_" + s for s in LOADS]
+SCRATCH.update({b: ("psum", [128, 512], F32) for b in ("d0", "d1", "d2", "d3", "wa", "wb", "wr", "ws")})
+LOADS = ["nx", "x0", "x1", "x2", "x3", "hi", "lo", "pin", "cu", "th", "fr0", "fr1", "q", "yq0", "yq1", "yq2", "yq3", "yp", "yn", "mf"]
+SEMAPHORES = (["dve", "act", "pe", "pool", "sent", "th"] + ["l_" + s for s in LOADS]
               + ["q%d_%d" % (p, c) for p in range(PH - 1) for c in range(NCH)] + ["b%d" % p for p in range(PH - 1)])
 
-CY, PCY, GA, SC, HOP = 0.00104, 0.00055, 1.55, 3.8, 0.10
-T_Q, T_B, T_CALL = 5.5, 5.0, 0.4
+CY, PCY, GA, SC = 0.00104, 0.00052, 1.55, 3.8
 ALL = slice(None)
 
 
+def X(buf, *idx, rows=ALL):
+    shape = SCRATCH[buf][1][1:]
+    starts, n = [0], 1
+    for k, size in enumerate(shape):
+        i = idx[k]
+        r = range(size)[i] if isinstance(i, slice) else range(i, i + 1)
+        n *= len(r)
+        if k < len(shape) - 1:
+            starts = [s * size + v for s in starts for v in r]
+        else:
+            runs = [(s * size + r[0], s * size + r[-1] + 1) for s in starts]
+    return (buf, (rows,) + idx, runs, set(range(128)[rows]), n)
+
+
 def A(buf, c0, c1, step=1):
-    return (buf, (ALL, slice(c0, c1, step)), c0, c1, None)
-
-
-def AX(buf, idx, lo, hi, rows=None):
-    return (buf, idx, lo, hi, rows)
+    return X(buf, slice(c0, c1, step))
 
 
 def width(a):
-    s = a[1][1]
-    return len(range(s.start, s.stop, s.step or 1))
+    return a[4]
 
 
 def two(*aps):
@@ -59,10 +72,10 @@ def two(*aps):
 
 
 def build_ops():
-    ops = []
+    ops, now = [], [""]
 
-    def add(name, cost, emit, reads, writes, kind="c", lat=0.0, sem=None, after=None):
-        ops.append({"name": name, "cost": cost, "emit": emit, "r": reads, "w": writes, "kind": kind, "lat": lat,
+    def add(name, cost, emit, reads, writes, kind="c", sem=None, after=None):
+        ops.append({"name": name, "p": now[0], "cost": cost, "emit": emit, "r": reads, "w": writes, "kind": kind,
                     "sem": sem, "after": after})
         return len(ops) - 1
 
@@ -82,7 +95,7 @@ def build_ops():
         n = width(out)
         cols = [s for s in (s1, s2) if isinstance(s, tuple)]
 
-        def emit(q, T, e, X):
+        def emit(q, T, e, R):
             if op1 is None:
                 return q.tensor_scalar(ap(T, out), ap(T, in0), sc(T, s1), None, op0)
             return q.tensor_scalar(ap(T, out), ap(T, in0), sc(T, s1), sc(T, s2), op0, op1)
@@ -90,29 +103,42 @@ def build_ops():
 
     def tt(name, out, in0, in1, op):
         k = 1 if "psum" in (SCRATCH[in0[0]][0], SCRATCH[in1[0]][0]) else 2
-        add(name, {"dve": cyc(k * width(out))}, lambda q, T, e, X: q.tensor_tensor(ap(T, out), ap(T, in0), ap(T, in1), op),
+        add(name, {"dve": cyc(k * width(out))}, lambda q, T, e, R: q.tensor_tensor(ap(T, out), ap(T, in0), ap(T, in1), op),
             [in0, in1], [out])
 
     def cp(name, out, in_):
         n = width(out)
-        add(name, {"dve": cyc(n / 2 if two(out, in_) else n)}, lambda q, T, e, X: q.tensor_copy(ap(T, out), ap(T, in_)),
+        add(name, {"dve": cyc(n / 2 if two(out, in_) else n)}, lambda q, T, e, R: q.tensor_copy(ap(T, out), ap(T, in_)),
             [in_], [out])
+
+    def affine(q, e, out, in_, scale, bias):
+        if e == "act":
+            if isinstance(bias, float) and bias == 0.0:
+                return q.activation(out, in_, AF.Copy, scale=scale)
+            return q.activation(out, in_, AF.Identity, bias=bias, scale=scale)
+        return q.tensor_scalar(out, in_, scale, bias, ALU.mult, ALU.add)
 
     def lin(name, out, in_, scale, bias):
         n = width(in_)
+        add(name, {"act": cyc(n), "dve": cyc(n / 2 if two(out, in_) else n)},
+            lambda q, T, e, R: affine(q, e, ap(T, out), ap(T, in_), sc(T, scale), sc(T, bias)),
+            [in_] + [s for s in (scale, bias) if isinstance(s, tuple)], [out])
 
-        def emit(q, T, e, X):
-            if e == "act":
-                if bias == 0.0:
-                    return q.activation(ap(T, out), ap(T, in_), AF.Copy, scale=scale)
-                return q.activation(ap(T, out), ap(T, in_), AF.Identity, bias=bias, scale=scale)
-            return q.tensor_scalar(ap(T, out), ap(T, in_), scale, bias, ALU.mult, ALU.add)
-        add(name, {"act": cyc(n), "dve": cyc(n / 2 if two(out, in_) else n)}, emit, [in_], [out])
+    def act(name, out, in_, func, scale, bias):
+        add(name, {"act": cyc(width(in_))}, lambda q, T, e, R: q.activation(ap(T, out), ap(T, in_), func, scale=scale, bias=sc(T, bias)),
+            [in_] + ([bias] if isinstance(bias, tuple) else []), [out])
 
-    def gather(name, out, win, off):
+    def same(name, out, in_, column):
+        apart = A("apart", 0, width(in_))
+        act(name + "a", apart, in_, AF.Abs, -1.0, column)
+        act(name, out, apart, AF.Relu, -1.0, 1.0)
+
+    def gather(name, out, win, off, scale=None, bias=None):
         n = 16 * width(off)
 
-        def emit(q, T, e, X):
+        def emit(q, T, e, R):
+            if scale is not None:
+                return affine(q, e, ap(T, out), ind(T, win, off), scale, bias)
             if e == "act":
                 return q.activation(ap(T, out), ind(T, win, off), AF.Copy)
             return q.tensor_copy(ap(T, out), ind(T, win, off))
@@ -120,10 +146,10 @@ def build_ops():
 
     def gtt(name, out, win, off, in1, op):
         add(name, {"dve": 0.05 + GA * 16 * width(off) * CY},
-            lambda q, T, e, X: q.tensor_tensor(ap(T, out), ind(T, win, off), ap(T, in1), op), [win, off, in1], [out])
+            lambda q, T, e, R: q.tensor_tensor(ap(T, out), ind(T, win, off), ap(T, in1), op), [win, off, in1], [out])
 
     def scatter(name, win, off, in_, in1=None):
-        def emit(q, T, e, X):
+        def emit(q, T, e, R):
             if in1 is None:
                 return q.tensor_copy(ind(T, win, off), ap(T, in_))
             return q.tensor_tensor(ind(T, win, off), ap(T, in_), ap(T, in1), ALU.add)
@@ -131,229 +157,267 @@ def build_ops():
 
     def scan(name, out, d0, d1, op0, op1):
         add(name, {"dve": cyc(width(out) / 2)},
-            lambda q, T, e, X: q.tensor_tensor_scan(ap(T, out), ap(T, d0), ap(T, d1), 0.0, op0, op1), [d0, d1], [out])
+            lambda q, T, e, R: q.tensor_tensor_scan(ap(T, out), ap(T, d0), ap(T, d1), 0.0, op0, op1), [d0, d1], [out])
 
-    def mm(name, parts, first=True, last=True):
-        def emit(q, T, e, X):
+    def mm(name, parts, group=None):
+        def emit(q, T, e, R):
             ins = None
             for k, (o, l, r) in enumerate(parts):
-                ins = q.matmul(ap(T, o), ap(T, l), ap(T, r), first and k == 0, last and k == len(parts) - 1)
+                ins = q.matmul(ap(T, o), ap(T, l), ap(T, r), me["first"] and k == 0, me["last"] and k == len(parts) - 1)
             return ins
-        add(name, {"pe": sum(max(64, width(o)) for o, l, r in parts) * PCY}, emit,
-            [x for o, l, r in parts for x in (l, r)], [o for o, l, r in parts])
+        me = ops[add(name, {"pe": sum(max(64, width(o)) for o, l, r in parts) * PCY}, emit,
+                     [x for o, l, r in parts for x in (l, r)], [o for o, l, r in parts])]
+        me.update({"group": group, "first": True, "last": True})
 
-    def wrap(name, bank, buf, c0, c1):
-        mm(name, [(A(bank, 0, (c1 - c0) // 16), A("zz", 15 - i, 143 - i), A(buf, c0 + i, c1, 16)) for i in range(16)])
+    def wrap(name, bank, z, buf, c0, c1):
+        mm(name, [(A(bank, 0, (c1 - c0) // 16), A(z, 15 - i, 143 - i), A(buf, c0 + i, c1, 16)) for i in range(16)])
 
     def memset(name, out, v):
-        add(name, {"dve": cyc(width(out) / 2 if two(out) else width(out))}, lambda q, T, e, X: q.memset(ap(T, out), v), [], [out])
+        add(name, {"dve": cyc(width(out) / 2 if two(out) else width(out))}, lambda q, T, e, R: q.memset(ap(T, out), v), [], [out])
 
     def iota(name, out, pat, base, cm):
-        def emit(q, T, e, X):
+        def emit(q, T, e, R):
             if SCRATCH[out[0]][2] == I32:
                 return q.iota(ap(T, out), pat, base, cm)
             return q.iota(ap(T, out), pat, base, cm, allow_small_or_imprecise_dtypes=True)
         add(name, {"pool": 0.16 + 2 * width(out) * CY}, emit, [], [out])
 
-    def load(sem, eng, out, src, lat, behind=()):
-        add("l_" + sem, {eng: 0.06}, lambda q, T, e, X: q.dma_start(ap(T, out), src(T)), list(behind), [out], "dma", lat, "l_" + sem)
+    def load(sem, eng, out, src, behind=()):
+        add("l_" + sem, {eng: 0.06}, lambda q, T, e, R: q.dma_start(ap(T, out), src(T)), list(behind), [out], "dma", "l_" + sem)
 
-    def move(sem, eng, out, in_, lat):
-        add("l_" + sem, {eng: 0.06}, lambda q, T, e, X: q.dma_start(ap(T, out), ap(T, in_)), [in_], [out], "dma", lat, "l_" + sem)
+    def move(sem, eng, out, in_):
+        add("l_" + sem, {eng: 0.06}, lambda q, T, e, R: q.dma_start(ap(T, out), ap(T, in_)), [in_], [out], "dma", "l_" + sem)
 
-    def store(sem, eng, dst, in_, lat):
-        add("l_" + sem, {eng: 0.06}, lambda q, T, e, X: q.dma_start(dst(T), ap(T, in_)), [in_], [], "dma", lat, "l_" + sem)
+    def store(sem, eng, dst, in_):
+        add("l_" + sem, {eng: 0.06}, lambda q, T, e, R: q.dma_start(dst(T), ap(T, in_)), [in_], [], "dma", "l_" + sem)
 
-    def send(sem, way, out, in_, lat):
-        def emit(q, T, e, X):
-            rid, pid, mask = X[way]
+    def send(name, sem, way, out, in_):
+        def emit(q, T, e, R):
+            rid, pid, mask = R[way]
             q.remote_dma(ap(T, out), ap(T, in_), T.sem[sem], T.sem.sent, pid, rid, mask)
-        k = add("s_" + sem, {"pool": T_CALL}, emit, [in_], [], "send")
-        add("r_" + sem, {}, way, [], [out], "recv", lat, sem, k)
+        k = add(name, {"pool": 0.3}, emit, [in_], [], "send")
+        add("r" + name, {}, way, [], [out], "recv", sem, k)
 
     def rows(buf, r, c1):
-        return AX(buf, (slice(r, 128, 16), slice(0, c1)), 0, c1, r)
+        return X(buf, slice(0, c1), rows=slice(r, 128, 16))
 
     def col(buf, k):
         return A(buf, k, k + 1)
 
     def nk(p, hop, k0, k1):
-        return AX("nk", (ALL, p, hop, slice(k0, k1)), 160 * p + 80 * hop + k0, 160 * p + 80 * hop + k1)
+        return X("nk", p, hop, slice(k0, k1))
+
+    def pu(row, k0, k1):
+        return X("pu", row, slice(k0, k1))
 
     xw, mw = A("xt", 0, W), A("mt", 0, W)
     id1, idn, blk = A("id1", 0, 128), A("idn", 0, 128), A("blk", 0, 128)
-    load("nx", "sp", A("nxs", 0, 256), lambda T: T.nx[:], 2.2)
-    load("pin", "act", A("pw", 0, 64), lambda T: T.pin[:], 2.2)
-    load("xa", "sp", A("xt", 0, W // 2), lambda T: T.x[:, 0:W // 2], 3.8)
-    load("cu", "act", A("cus", 0, 16), lambda T: T.cu[:], 2.2)
-    memset("z_mt", A("mt", 0, W // 2), 0.0)
-    lin("z_mt2", A("mt", W // 2, W), A("mt", 0, W // 2), 1.0, 0.0)
-    cp("hi", A("hi", 0, 256), A("nxs", 0, 256))
-    tt("lo", A("lo", 0, 256), A("nxs", 0, 256), A("hi", 0, 256), ALU.subtract)
-    move("hi", "sp", rows("mt", 0, W), A("hi", 0, 256), 2.2)
-    move("lo", "sp", rows("mt", 1, W), A("lo", 0, 256), 2.2)
-    load("xb", "sp", A("xt", W // 2, W), lambda T: T.x[:, W // 2:W], 3.6, [A("hi", 0, 256)])
-    load("q", "sp", A("qin", 0, 1024), lambda T: T.q[:], 3.6, [A("lo", 0, 256)])
-    load("th", "sp", A("ths", 0, 64), lambda T: T.th[:], 2.2)
-    memset("z_fr", A("frs", 0, RG), 0)
-    load("fr0", "sp", rows("frs", 0, RG), lambda T: T.fr[:], 2.2)
-    load("fr1", "sp", rows("frs", 1, RG), lambda T: T.fr[:], 2.2)
+    hi, lo = A("dg", 0, 256), A("dg", 256, 512)
+    load("nx", "sp", A("nxs", 0, 256), lambda T: T.nx[:])
+    load("pin", "act", X("pw", 0, ALL), lambda T: T.pin[:])
+    load("cu", "act", A("cus", 0, 16), lambda T: T.cu[:])
+    for k in range(4):
+        load("x%d" % k, "sp", A("xt", k * W // 4, (k + 1) * W // 4), lambda T, k=k: T.x[:, k * W // 4:(k + 1) * W // 4])
+    memset("z0", A("mt", 0, W // 4), 0.0)
+    memset("z1", A("mt", W // 4, W // 2), 0.0)
+    for k in (2, 3):
+        lin("z%d" % k, A("mt", k * W // 4, (k + 1) * W // 4), A("mt", 0, W // 4), 1.0, 0.0)
+    cp("hi", hi, A("nxs", 0, 256))
+    tt("lo", lo, A("nxs", 0, 256), hi, ALU.subtract)
+    move("hi", "sp", rows("mt", 0, W), hi)
+    move("lo", "sp", rows("mt", 1, W), lo)
+    load("q", "sp", A("qraw", 0, 1024), lambda T: T.q[:])
+    load("th", "sp", A("ths", 0, 64), lambda T: T.th[:])
+    memset("zfr", A("frs", 0, RG), 0)
+    for r in range(2):
+        load("fr%d" % r, "sp", rows("frs", r, RG), lambda T: T.fr[:])
     iota("i_p", col("ci", 0), [[0, 1]], 0, 1)
     iota("i_pf", col("cf", 0), [[0, 1]], 0, 1)
     iota("i_y", A("ioy", 0, 144), [[1, 144]], 0, 0)
+    iota("i_j", A("ioj", 0, 64), [[HF, 2], [16, 32]], 0, 0)
     iota("i_l", A("iol", 0, 9), [[0, 3], [4, 3]], 0, 0)
     iota("i_g", A("iog", 0, 128), [[1, 8], [0, 16]], 0, 0)
     iota("i_w", A("iow", 0, 3 * RG), [[0, 3], [1, RG]], 0, 0)
-    iota("i_k", A("keep", 0, 144), [[0, 36], [1, 4]], 0, 0)
+    iota("i_k", A("keep", 0, 288), [[0, 36], [1, 8]], 0, 0)
     iota("i_e", A("ee", 0, 36), [[16, 36]], 257, 1)
     ts("c_g", col("ci", 1), col("ci", 0), 4, ALU.logical_shift_right)
     ts("c_zc", col("cf", 1), col("ci", 1), 16.0, ALU.mult, 15.0, ALU.add)
-    ts("c_z", A("zz", 0, 144), A("ioy", 0, 144), col("cf", 1), ALU.is_equal)
+    same("c_z", A("zz", 0, 144), A("ioy", 0, 144), col("cf", 1))
     lin("c_z8", A("z8", 0, 144), A("zz", 0, 144), 8192.0, 0.0)
+    lin("c_zf", A("zf", 0, 144), A("zz", 0, 144), 1.0 / W, 0.0)
+    same("c_id", id1, A("ioy", 0, 128), col("cf", 0))
+    lin("c_idn", idn, id1, -1.0, 0.0)
+    if any(SILU):
+        act("c_idk", A("idk", 0, 128), id1, AF.Silu, 2048.0, 0.0)
+        ops[-1]["cost"]["act"] += 1.3
+    else:
+        lin("c_idk", A("idk", 0, 128), id1, 2048.0, 0.0)
+    ts("c_i", col("ci", 4), col("ci", 0), 15, ALU.bitwise_and)
+    cp("c_if", col("cf", 9), col("ci", 4))
+    lin("c_j", A("jc", 0, 64), A("ioj", 0, 64), 1.0, col("cf", 9))
     ts("c_b", col("ci", 2), col("ci", 0), 3, ALU.bitwise_and)
     ts("c_a", col("ci", 3), col("ci", 0), 2, ALU.logical_shift_right, 3, ALU.bitwise_and)
     cp("c_af", col("cf", 3), col("ci", 3))
     ts("c_h", col("cf", 5), col("ci", 2), 16.0, ALU.mult, col("cf", 3), ALU.add)
     ts("c_l1", A("l1", 0, 9), A("iol", 0, 9), col("cf", 5), ALU.add)
     ts("c_l2", A("l2", 0, 3), A("iol", 0, 3), col("cf", 3), ALU.add)
-    ts("c_i", col("ci", 4), col("ci", 0), 15, ALU.bitwise_and)
     ts("c_m1", col("cf", 6), col("ci", 4), 1.0, ALU.is_equal)
     ts("c_m0", col("cf", 7), col("ci", 4), 0.0, ALU.is_equal, 2.0 * W, ALU.mult)
-    cp("c_if", col("cf", 9), col("ci", 4))
-    ts("c_wi", A("wi", 0, 12), A("ioy", 0, 12), 16.0, ALU.mult, col("cf", 9), ALU.add)
+    lin("c_wi", A("wi", 0, 12), A("ioy", 0, 12), 16.0, col("cf", 9))
     cp("c_gf", col("cf", 8), col("ci", 1))
-    ts("c_id", id1, A("ioy", 0, 128), col("cf", 0), ALU.is_equal)
-    lin("c_idn", idn, id1, -1.0, 0.0)
-    lin("c_idk", A("idk", 0, 128), id1, 2048.0, 0.0)
-    ts("c_blk", blk, A("iog", 0, 128), col("cf", 8), ALU.is_equal)
-    ts("c_gt0", A("gt0", 0, 128), A("ioy", 0, 128), col("cf", 0), ALU.is_lt, -1.0, ALU.mult)
-    tt("c_gtn", A("gtn", 0, 128), A("gt0", 0, 128), blk, ALU.mult)
-    ts("c_fb", A("fb", 2048, 2048 + 3 * RG), A("iow", 0, 3 * RG), col("cf", 6), ALU.mult, col("cf", 7), ALU.add)
-    memset("c_m128", A("m128", 0, RG), -128.0)
-    cp("pinu", A("pu", 0, 64), A("pw", 0, 64))
-    cp("cuu", A("pu", 64, 76), A("cus", 0, 12))
-    ts("cu4", A("a4", 0, 12), A("cus", 0, 12), float(W), ALU.add)
+    same("c_blk", blk, A("iog", 0, 128), col("cf", 8))
+    lin("c_gt0", A("gt0", 0, 128), blk, -1.0, 0.0)
+    add("c_gtn", {"pool": 0.21 + 256 * CY},
+        lambda q, T, e, R: q.affine_select(T.gtn[:], T.gt0[:], [[-1, 128]], ALU.is_gt, 0.0, 0, 1), [A("gt0", 0, 128)], [A("gtn", 0, 128)])
+    lin("c_fb", A("fb", 2048, 2048 + 3 * RG), A("iow", 0, 3 * RG), col("cf", 6), col("cf", 7))
+    for p in range(PH - 1):
+        if SILU[p]:
+            lin("c_fw%d" % p, A("fw", 2048 + RG * p, 2048 + RG * p + RG), A("fb", 2048, 2048 + RG), 1.0, 64.0)
+    lin("c_m128", A("m128", 0, RG), A("mt", 0, RG), 0.0, -128.0)
+    lin("c_va", A("valid", 0, 12), A("ioy", 0, 12), 0.0, 1.0)
+    cp("pinu", pu(0, 12, 76), X("pw", 0, ALL))
+    cp("cuu", pu(0, 0, 12), A("cus", 0, 12))
+    ts("cu4", A("a4", 0, 12), A("cus", 0, 12), 1.0 / W, ALU.mult, 1.0, ALU.add)
     ts("th8", A("th8", 0, 64), A("ths", 0, 64), 8192.0, ALU.mult)
+    send("st", "th", "b", A("thn", 0, 64), A("th8", 0, 64))
     ts("fr_t", A("frt", 0, RG), A("frs", 0, RG), col("cf", 6), ALU.mult)
     tt("fr_d", A("f0", 0, RG), A("frs", 0, RG), A("frt", 0, RG), ALU.subtract)
+    for h, H in enumerate("AB"):
+        lin("q" + H, A("qin", HF * h, HF * h + HF), A("qraw", HF * h, HF * h + HF), SCL[0], SCL[0] * QB[0])
+
+    def release(p):
+        K = p + 1
+        n8, n1 = 96 * K, 12 * K
+        tt("bit", A("bin", 64 * p, 64 * p + 64), A("kin", 64 * p, 64 * p + 64), A("thn", 0, 64), ALU.is_ge)
+        gtt("mo", A("hm", 288 * K + 1, 288 * K + n8, 2), A("bin", 64 * p, 64 * p + 64), A("l1", 0, 3 * K),
+            A("hm", 288 * p, 288 * p + n8, 2), ALU.mult)
+        scan("ho", A("ho", 0, n8), A("keep", 0, n8), A("hm", 288 * K, 288 * K + n8), ALU.mult, ALU.max)
+        rel, cum = A("rel", 0, n1), A("cum", 0, n1)
+        tt("rel", rel, A("valid", 0, n1), A("ho", 7, n8, 8), ALU.is_gt)
+        scan("cum", cum, rel, rel, ALU.add, ALU.max)
+        mm("rk", [(A("ws", 0, n1), A("gtn", 0, 128), rel), (A("ws", 0, n1), A("idk", 0, 128), rel),
+                  (A("ws", 0, n1), blk, cum), (A("ws", 40, 41), blk, A("cum", n1 - 1, n1))])
+        tt("pos", A("pos", 0, n1), A("ws", 0, n1), A("ee", 0, n1), ALU.max)
+        ts("posu", A("posu", 0, n1), A("pos", 0, n1), -1.0, ALU.add)
+        if p < PH - 2:
+            tt("vv", A("valid", 0, n1), A("valid", 0, n1), rel, ALU.subtract)
+        va = A("valid", n1, n1 + 12)
+        ts("ac", va, A("wi", 0, 12), A("ws", 40, 41), ALU.is_lt)
+        tt("ad", A("mx", 0, 12), A("a4", 16 * K, 16 * K + 12), va, ALU.subtract)
+        ts("au", A("au", 16 * K, 16 * K + 12), A("mx", 0, 12), float(W), ALU.mult)
+        for k in range(K):
+            off = A("posu", 12 * k, 12 * k + 12)
+            if not SILU[p]:
+                scatter("sl%d" % k, A("fb", RG * p, RG * p + 2048 + RG), off, A("g0", 1216 * k, 1216 * k + RG))
+                continue
+            win, src = A("fw", RG * p, RG * p + 2048 + RG), A("fs", RG * k, RG * k + RG)
+            add("sl%d" % k, {"act": 0.05 + SC * RG * CY},
+                lambda q, T, e, R, win=win, off=off, src=src: q.activation(ind(T, win, off), ap(T, src), AF.Silu), [off, src], [win])
+        if SILU[p]:
+            ts("fr", A("fb", 2048 + RG * p, 2048 + RG * K), A("fw", 2048 + RG * p, 2048 + RG * K), RND, ALU.add, RND + 64.0, ALU.subtract)
 
     for p in range(PH):
+        now[0] = p
         last = p == PH - 1
-        fbuf, fc = ("f0", 0) if p == 0 else ("fb", 2048 + RG * (p - 1))
-        U, G, K, XC = 80 * p, 1216 * p, p + 1, 2240 * (p % 2)
+        free = A("f0", 0, RG) if p == 0 else A("fb", 2048 + RG * (p - 1), 2048 + RG * p)
+        s, G, r0 = SCL[p], 1216 * p, A("wr", 0, RG)
         fu, au, a4 = A("fu", 16 * p, 16 * p + 12), A("au", 16 * p, 16 * p + 12), A("a4", 16 * p, 16 * p + 12)
         if p == 0:
-            au = A("pu", 64, 76)
-        fw = A("ws", 0, 12)
-        wrap("wf%d" % p, "ws", fbuf, fc, fc + RG)
-        cp("fu%d" % p, fu, fw)
+            au = pu(0, 0, 12)
+        XH = [2 * HF * (h + 2 * (p % 2)) for h in range(2)]
+        for h, H in enumerate("AB"):
+            bank, k0, k1 = ("wa", 0, 44) if h == 0 else ("wb", 44, 76)
+            n1u, n2u = A("n1u", 80 * p + k0, 80 * p + k1), A("n2u", 64 * p + 32 * h, 64 * p + 32 * h + 32)
+            gather("g0" + H, A("g0", G + 16 * k0, G + 16 * k1), mw, pu(2 * p, k0, k1))
+            wrap("w0" + H, bank, "zz", "g0", G + 16 * k0, G + 16 * k1)
+            cp("nu0" + H, n1u, A(bank, 0, k1 - k0))
+            lin("nk0" + H, nk(p, 0, k0, k1), A(bank, 0, k1 - k0), 1.0, 0.0)
+            gather("g1" + H, A("g1", 16 * k0, 16 * k1), mw, n1u)
+            wrap("w1" + H, bank, "zz", "g1", 16 * (k1 - 32), 16 * k1)
+            cp("nu1" + H, n2u, A(bank, 0, 32))
+            lin("nk1" + H, nk(p, 1, k1 - 32, k1), A(bank, 0, 32), 1.0, float(W))
+            gather("x1" + H, A("xh", XH[h], XH[h] + HF), xw, A("n1u", 80 * p + k1 - 32, 80 * p + k1), s, s * (TB[p] - 0.5))
+            gather("x2" + H, A("xh", XH[h] + HF, XH[h] + 2 * HF), xw, n2u, s, s * (TB[p] - 0.5))
+        if any(SILU[p:]):
+            lin("s32", A("fs", RG * p, RG * p + RG), A("g0", G, G + RG), 1.0, 64.0)
         if not last:
-            tt("mn%d" % p, A("mn", 0, 12), fw, a4, ALU.min)
-            ts("va%d" % p, A("valid", 12 * p, 12 * p + 12), fw, float(W), ALU.is_lt)
-            ts("an%d" % p, A("an", 0, 12), A("mn", 0, 12), W - 1, ALU.bitwise_and)
-            cp("anu%d" % p, A("pu", U + 144, U + 156), A("an", 0, 12))
-            ts("a4%d" % p, A("a4", 16 * p + 16, 16 * p + 28), A("an", 0, 12), float(W), ALU.add)
-        for h, (ca, cb) in enumerate(PRE[p]):
-            k0, k1 = 16 * ca, 16 * cb
-            ke = k1 + (12 if cb == NCH else 0)
-            bank = "wa" if h % 2 == 0 else "wb"
-            nm = "%d_%d" % (p, h)
-            gather("g1_" + nm, A("g1", G + 16 * k0, G + 16 * ke), mw, A("pu", U + k0, U + ke))
-            wrap("w1_" + nm, bank, "g1", G + 16 * k0, G + 16 * ke)
-            cp("n1u_" + nm, A("n1u", U + k0, U + ke), A(bank, 0, ke - k0))
-            lin("nk1_" + nm, nk(p, 0, k0, ke), A(bank, 0, ke - k0), 1.0, 0.0)
-            gather("g2_" + nm, A("g2", G + 16 * k0, G + 16 * ke), mw, A("n1u", U + k0, U + ke))
-            wrap("w2_" + nm, bank, "g2", G + 16 * k0, G + 16 * k1)
-            cp("n2u_" + nm, A("n2u", 64 * p + k0, 64 * p + k1), A(bank, 0, k1 - k0))
-            lin("nk2_" + nm, nk(p, 1, k0, k1), A(bank, 0, k1 - k0), 1.0, float(W))
-            kx = k1 if last else ke
-            gather("x1_" + nm, A("x12", XC + 16 * k0, XC + 16 * kx), xw, A("n1u", U + k0, U + kx))
-            gather("x2_" + nm, A("x12", XC + 1216 + 16 * k0, XC + 1216 + 16 * k1), xw, A("n2u", 64 * p + k0, 64 * p + k1))
-        if not last:
-            gather("xa%d" % p, A("xab", 0, RG), xw, A("pu", U + 64, U + 76))
-            mm("xs%d" % p, [(A("ws", 0, RG), id1, A("xab", 0, RG)), (A("ws", 0, RG), id1, A("x12", XC + 1024, XC + 1216))])
-            lin("xv%d" % p, A("xv", RG * p, RG * p + RG), A("ws", 0, RG), 0.5, 127.75)
-            scatter("sa%d" % p, A("mt", 0, TW), au, A(fbuf, fc, fc + RG))
-            scatter("sf%d" % p, A("mt", 0, TW), fu, A("g2", G + 1024, G + 1216))
+            gather("xa", A("xab", 0, RG), xw, pu(2 * p, 0, 12))
+            gather("xb", A("xab", RG, 2 * RG), xw, A("n1u", 80 * p, 80 * p + 12))
+            mm("xs", [(r0, id1, A("xab", 0, RG)), (r0, id1, A("xab", RG, 2 * RG))])
+            lin("xv", A("xv", 0, RG), r0, 0.5, 127.75)
         else:
-            mm("wn", [(A("wa", 0, 256), A("zz", 15 - i, 143 - i), A("mt", 256 * i, 256 * i + 256)) for i in range(16)])
-            lin("ynf", A("ynf", 0, 256), A("wa", 0, 256), 1.0, 0.0)
-            move("mf", "sp", rows("mf", 0, W), A("ynf", 0, 256), 2.6)
-            mm("nbs", [(A("wb", 0, RG), blk, A("g2", G + 1024, G + 1216))])
-            lin("nbf", A("ff", RG, 2 * RG), A("wb", 0, RG), 1.0, 0.0)
-            mm("fs", [(A("wb", 0, RG), blk, A(fbuf, fc, fc + RG))])
-            lin("ff", A("ff", 0, RG), A("wb", 0, RG), 1.0, 0.0)
-            scatter("sa%d" % p, A("mf", 0, TW), au, A("ff", 0, RG))
-            scatter("sf%d" % p, A("mf", 0, TW), fu, A("ff", RG, 2 * RG))
-        for h, (ca, cb) in enumerate(RD[p]):
-            for c in range(ca, cb):
-                nm = "%d_%d" % (p, c)
-                bank, xc, qa = "d%d" % c, XC + CH * c, A("qin", 1024 * p + CH * c, 1024 * p + CH * c + CH)
-                mm("dx" + nm, [(A(bank, 0, CH), id1, A("x12", xc, xc + CH)),
-                               (A(bank, CH, 2 * CH), id1, A("x12", xc + 1216, xc + 1216 + CH))], True, False)
-                mm("dq" + nm, [(A(bank, 0, CH), idn, qa), (A(bank, CH, 2 * CH), idn, qa)], False, True)
-                ab = AX("ab", (ALL, ALL, slice(CH * c, CH * c + CH)), CH * c, CH * c + CH)
-                add("abs" + nm, {"act": cyc(512)},
-                    lambda q, T, e, X, ab=ab, bank=bank, p=p: q.activation(ap(T, ab), T[bank][:, 0:512], AF.Abs, bias=128.0 if p else 0.0),
-                    [A(bank, 0, 512)], [ab])
-            nm, k0, k1, n = "%d_%d" % (p, h), 16 * ca, 16 * cb, 16 * (cb - ca)
-            mm("wd" + nm, [(A("wd", 0, 2 * n), A("z8", 15 - i, 143 - i),
-                            AX("ab", (ALL, ALL, slice(CH * ca + i, CH * cb, 16)), CH * ca, CH * cb)) for i in range(16)])
-            tt("key" + nm, A("key", 2 * k0, 2 * k1), A("wd", 0, 2 * n),
-               AX("nk", (ALL, p, ALL, slice(k0, k1)), 160 * p + k0, 160 * p + 80 + k1), ALU.add)
-            km = A("km", 64 * p + k0, 64 * p + k1)
-            tt("min" + nm, km, A("key", 2 * k0, 2 * k0 + n), A("key", 2 * k0 + n, 2 * k1), ALU.min)
-            ts("and" + nm, A("pw", 64 * p + 64 + k0, 64 * p + 64 + k1), km, W - 1, ALU.bitwise_and)
-            cp("pu" + nm, A("pu", U + 80 + k0, U + 80 + k1), A("pw", 64 * p + 64 + k0, 64 * p + 64 + k1))
-            if cb == NCH and not last:
-                tt("bit%d" % p, A("bout", 64 * p, 64 * p + 64), A("km", 64 * p, 64 * p + 64), A("th8", 0, 64), ALU.is_ge)
-                send("b%d" % p, "b", A("bin", 64 * p, 64 * p + 64), A("bout", 64 * p, 64 * p + 64), T_B)
-            for sa, sz in SG[p]:
-                if not ca <= sa < cb:
-                    continue
-                nm, q0, q1 = "%d_%d" % (p, sa), 1024 * p + CH * sa, 1024 * p + CH * sz
-                ss = A("ss", CH * sa, CH * sz)
-                gtt("sg" + nm, ss, xw, A("pu", U + 80 + 16 * sa, U + 80 + 16 * sz), A("qin", q0, q1), ALU.add)
-                lin("half" + nm, A("qout", q0, q1), ss, 0.5, 63.75 if p else 127.75)
+            o = A("wr", 0, 256)
+            mm("wn", [(o, A("zz", 15 - i, 143 - i), A("mt", 256 * i, 256 * i + 256)) for i in range(16)])
+            lin("ynf", A("ynf", 0, 256), o, 1.0, 0.0)
+            move("mf", "sp", rows("mf", 0, W), A("ynf", 0, 256))
+            mm("nbs", [(r0, blk, A("g1", 0, RG))])
+            lin("nbf", A("ff", RG, 2 * RG), r0, 1.0, 0.0)
+        if p:
+            release(p - 1)
+        fw = A("ws", 0, 12)
+        wrap("wf", "ws", "zf", free[0], free[2][0][0], free[2][0][1])
+        ts("fu", fu, fw, float(W), ALU.mult)
+        if not last:
+            tt("mn", A("mn", 0, 12), fw, a4, ALU.min)
+            a4n = A("a4", 16 * p + 16, 16 * p + 28)
+            tt("a4", a4n, A("mn", 0, 12), A("valid", 12 * p, 12 * p + 12), ALU.add)
+            ts("anu", pu(2 * p + 2, 0, 12), a4n, -1.0, ALU.add, float(W), ALU.mult)
+            scatter("sa", A("mt", 0, TW), au, free)
+            scatter("sf", A("mt", 0, TW), fu, A("g1", 0, RG))
+            scatter("sx", A("xt", 0, TW), fu, A("xv", 0, RG), A("m128", 0, RG))
+        else:
+            mm("fs", [(r0, blk, free)])
+            lin("ff", A("ff", 0, RG), r0, 1.0, 0.0)
+            scatter("sf", A("mf", 0, TW), fu, A("ff", RG, 2 * RG))
+            scatter("sa", A("mf", 0, TW), au, A("ff", 0, RG))
+        for h, H in enumerate("AB"):
+            b, bank = XH[h], "wa" if h == 0 else "wb"
+            for u in range(2):
+                d, c = "d%d" % (2 * h + u), 2 * h + u
+                if MODE[p] == "hop":
+                    nm, ab = "%d%s" % (u + 1, H), X("ab", u, slice(HF * h, HF * h + HF))
+                    mm("dq" + nm, [(A(d, 0, HF), idn, A("qin", 1024 * p + HF * h, 1024 * p + HF * h + HF))], (p, d))
+                    mm("dx" + nm, [(A(d, 0, HF), id1, A("xh", b + HF * u, b + HF * u + HF))], (p, d))
+                else:
+                    nm, ab = "%d" % c, X("ab", ALL, slice(CH * c, CH * c + CH))
+                    qa = A("qin", 1024 * p + CH * c, 1024 * p + CH * c + CH)
+                    for hop in range(2):
+                        xc = b + HF * hop + CH * u
+                        mm("dx%d%d" % (hop + 1, c), [(A(d, CH * hop, CH * hop + CH), id1, A("xh", xc, xc + CH))], (p, d))
+                    mm("dq" + nm, [(A(d, 0, CH), idn, qa), (A(d, CH, 2 * CH), idn, qa)], (p, d))
+                add("ab" + nm, {"act": cyc(HF)},
+                    lambda q, T, e, R, ab=ab, d=d, p=p: q.activation(ap(T, ab), T[d][:, 0:HF], AF.Abs, scale=1.0 / SCL[p],
+                                                                     bias=QB[p] - TB[p] + 0.5), [A(d, 0, HF)], [ab])
+            ks = slice(32 * h, 32 * h + 32)
+            mm("wd" + H, [(A(bank, 0, 64), A("z8", 15 - i, 143 - i), X("ab", ALL, slice(HF * h + i, HF * h + HF, 16))) for i in range(16)])
+            tt("ka" + H, X("key", 2 * h, ALL, ALL), A(bank, 0, 64), X("nk", p, ALL, slice(32 * h + 12, 32 * h + 44)), ALU.add)
+            tt("kb" + H, X("key", 2 * h + 1, ALL, ALL), A(bank, 0, 64), A("jc", 0, 64), ALU.add)
+            km = X("km", slice(2 * p, 2 * p + 2), ks)
+            tt("min" + H, km, X("key", slice(2 * h, 2 * h + 2), 0, ALL), X("key", slice(2 * h, 2 * h + 2), 1, ALL), ALU.min)
+            pw = X("pw", slice(2 * p + 2, 2 * p + 4), ks)
+            ts("and" + H, pw, km, W - 1, ALU.bitwise_and)
+            cp("pu" + H, X("pu", slice(2 * p + 2, 2 * p + 4), slice(32 * h + 12, 32 * h + 44)), pw)
+            if h == 1 and not last:
+                send("sb", "b%d" % p, "b", A("kin", 64 * p, 64 * p + 64), X("km", 2 * p, ALL))
+            step = LAST[h] if last else 1
+            for c in range(2 * h, 2 * h + 2, step):
+                q0, q1 = 1024 * p + CH * c, 1024 * p + CH * (c + step)
+                out = A("ss", CH * c, CH * (c + step)) if last else A("qout", q0, q1)
+                gtt("sg%d" % c, out, A("xh", b, b + 2 * HF), pu(2 * p + 3, 12 + 16 * c, 12 + 16 * (c + step)), A("qin", q0, q1), ALU.add)
                 if last:
-                    lin("fin" + nm, A("qout", q0 + 1024, q1 + 1024), A("qout", q0, q1), 1.0, -128.0)
-                    continue
-                for c in range(sa, sz):
-                    qc = 1024 * p + CH * c
-                    send("q%d_%d" % (p, c), c, A("qin", qc + 1024, qc + 1024 + CH), A("qout", qc, qc + CH), T_Q)
+                    ts("fin%d" % c, A("qout", q0, q1), out, RND, ALU.add, RND + 1.0, ALU.subtract)
+                    store("yq%d" % c, "sp", lambda T, c=c, step=step: T.yq[:, CH * c:CH * (c + step)], A("qout", q0, q1))
+                else:
+                    send("sq%d" % c, "q%d_%d" % (p, c), c, A("qin", q0 + 1024, q1 + 1024), A("qout", q0, q1))
         if last:
             break
-        scatter("sx%d" % p, A("xt", 0, TW), fu, A("xv", RG * p, RG * p + RG), A("m128", 0, RG))
-        n4, n1 = 48 * K, 12 * K
-        gather("rx%d" % p, A("retx", 48 * p, n4), nk(p, 0, 64, 76), A("l2", 0, 3))
-        l1 = A("l1", 0, 3 * K)
-        eqo, eqn = A("eq", 144 * p, 144 * p + n4), A("eq", 144 * K, 144 * K + n4)
-        gtt("eqo%d" % p, A("eq", 192 * p, 192 * p + 48), A("pw", 64 * p, 64 * p + 64), A("l1", 0, 3), A("retx", 48 * p, n4), ALU.is_equal)
-        gtt("eqn%d" % p, eqn, A("pw", 64 * p + 64, 64 * p + 128), l1, A("retx", 0, n4), ALU.is_equal)
-        scan("hn%d" % p, A("hn", 0, n4), A("keep", 0, n4), eqn, ALU.mult, ALU.max)
-        tt("v2%d" % p, A("v2", 0, n1), A("valid", 0, n1), A("hn", 3, n4, 4), ALU.is_gt)
-        gtt("mo%d" % p, A("mo", 0, n4), A("bin", 64 * p, 64 * p + 64), l1, eqo, ALU.mult)
-        scan("ho%d" % p, A("ho", 0, n4), A("keep", 0, n4), A("mo", 0, n4), ALU.mult, ALU.max)
-        rel, cum = A("rel", 0, n1), A("cum", 0, n1)
-        tt("rel%d" % p, rel, A("v2", 0, n1), A("ho", 3, n4, 4), ALU.is_gt)
-        scan("cum%d" % p, cum, rel, rel, ALU.add, ALU.max)
-        mm("rk%d" % p, [(A("ws", 0, n1), A("gtn", 0, 128), rel), (A("ws", 0, n1), A("idk", 0, 128), rel),
-                        (A("ws", 0, n1), blk, cum), (A("ws", 40, 41), blk, A("cum", n1 - 1, n1))])
-        tt("pos%d" % p, A("pos", 0, n1), A("ws", 0, n1), A("ee", 0, n1), ALU.max)
-        ts("posu%d" % p, A("posu", 0, n1), A("pos", 0, n1), -1.0, ALU.add)
-        ts("ac%d" % p, A("mx", 0, 12), A("wi", 0, 12), A("ws", 40, 41), ALU.is_lt, -float(W), ALU.mult)
-        tt("ad%d" % p, A("mx", 16, 28), A("mx", 0, 12), A("a4", 16 * p + 16, 16 * p + 28), ALU.add)
-        cp("au%d" % p, A("au", 16 * p + 16, 16 * p + 28), A("mx", 16, 28))
-        if p < PH - 2:
-            tt("vv%d" % p, A("valid", 0, n1), A("valid", 0, n1), rel, ALU.subtract)
-        for k in range(K):
-            scatter("sl%d_%d" % (p, k), A("fb", RG * p, RG * p + 2048 + RG), A("posu", 12 * k, 12 * k + 12),
-                    A("g1", 1216 * k + 1024, 1216 * k + 1216))
-    store("yq0", "sp", lambda T: T.yq[:, 0:512], A("qout", 4096, 4608), 2.6)
-    store("yq1", "sp", lambda T: T.yq[:, 512:1024], A("qout", 4608, 5120), 2.6)
-    cp("ypf", A("ypf", 0, 64), A("pw", 256, 320))
-    store("yp", "sp", lambda T: T.yp[:], A("ypf", 0, 64), 2.2)
-    store("yn", "sp", lambda T: T.yn[:], rows("mf", 0, W), 2.6)
+        K = p + 1
+        gather("rx", A("retx", 48 * p, 48 * K), nk(p, 0, 0, 12), A("l2", 0, 3))
+        gtt("eqo", A("hm", 384 * p, 384 * p + 96, 2), X("pw", 2 * p, ALL), A("l1", 0, 3), A("retx", 48 * p, 48 * K), ALU.is_equal)
+        gtt("eqn", A("hm", 288 * K, 384 * K, 2), X("pw", 2 * p + 2, ALL), A("l1", 0, 3 * K), A("retx", 0, 48 * K), ALU.is_equal)
+    cp("ypf", A("ypf", 0, 64), X("pw", 8, ALL))
+    store("yp", "sp", lambda T: T.yp[:], A("ypf", 0, 64))
+    store("yn", "sp", lambda T: T.yn[:], rows("mf", 0, W))
     return ops
 
 
@@ -362,15 +426,18 @@ def meet(a, b):
         return False
     if SCRATCH[a[0]][0] == "psum":
         return True
-    return a[2] < b[3] and b[2] < a[3] and (a[4] is None or b[4] is None or a[4] == b[4])
+    return bool(a[3] & b[3]) and any(x0 < y1 and y0 < x1 for x0, x1 in a[2] for y0, y1 in b[2])
 
 
 def find_deps(ops):
     deps = []
     for k, o in enumerate(ops):
         d = {}
+        mine = {a[0] for a in o["r"] + o["w"]}
         for j in range(k):
             e = ops[j]
+            if not any(b[0] in mine for b in e["r"] + e["w"]) or o.get("group") and o["group"] == e.get("group"):
+                continue
             if any(meet(a, b) for a in o["r"] + o["w"] for b in e["w"]) or any(meet(a, b) for a in o["w"] for b in e["r"]):
                 d[j] = False
             elif any(SCRATCH[a[0]][0] == "psum" and meet(a, b) for a in o["r"] for b in e["r"]):
@@ -381,33 +448,57 @@ def find_deps(ops):
     return deps
 
 
-ORDER = """
-17 16 21 0 4 13 2 5 12 1a 6 7 20 24 25 51 3a 34 48 14 15 35 52 19 8 53 39 18 26 50 9 10 27 54 40 41 49 71a 61 62 37 72 63 55 65a
-64 73 75 74a 66 67 69a 22 70a 23 42 11 28 76 77 79 80a 89 90 84 91a 86 87 88a 78a 56 105 108 68a 106 107a 81a 85 92 93 29 94 95
-96 97 109 110a 101 111 98 112 57 113 58 114 59 115 116 123 47 152a 153 124 30 119 99 154 31 120 33 43 102a 82 162a 163 44 128 32
-45 83a 164 165 155a 156a 157 127 166a 130 158 161a 129 160 167 131 168 170 103 117 118 177 180 104 133 132 134 125 100 178 38 135
-121 36 171a 181 136 199 46 137 138 60 169a 140 139 141 196 144 179a 182a 126 142 159a 122 200 201a 183 184 197 175 145 185 146
-147 198a 202 176 203 186 204 187 207 205 149 188 148 150 206 192 210 193 172a 173 214 211 244a 245 246 189a 174a 218 215 254a 255
-247 256 248a 219 208 221 258 143 249 222 257 250 252a 190 194 220 223 212 262a 191 259 253a 209 224 225 226 227 216 228 260 263a
-269 272 264a 270 271a 151 213 195 291 273 229 231 274a 230 232 288 235 233 311a 261a 217 289 290a 236 267 237 238 292 239 268
-251a 275 276 241 293a 294 277 278 279 240 295 296 297 299 284 300 331a 332 285a 280 298 242 281a 286 333 335a 302 341 306 334a
-265 336 337 307 338 342 234 343 313 303a 266a 310 345a 282 287 312 349 301 314 304 316 344a 340a 315 317 318 319 351 339a 346
-352a 305 347 348 320 321 363 323 322 243 350a 326 327 324 364 365a 283 360 361 377 362a 374 308 375 366 328 367 325 368 369 370
-376a 309 378 379a 354 355a 371 380 381 329 356 372a 353 357a 373a 382 383 384 385 388 330 358 359 386a 387a 389 392 390 391
-"""
+QUEUES = {
+    "sp": """
+        l_nx l_q l_fr1 l_th l_fr0 l_x1 l_hi l_lo l_x0 l_x3 l_x2 l_mf.3 l_yn.3 l_yp.3 l_yq0.3 l_yq1.3 l_yq3.3 l_yq2.3""",
+    "pool": """
+        i_j i_pf i_p i_k i_g i_l i_y i_w st sb.0 sq0.0 sq1.0 sq2.0 sq3.0 c_gtn i_e sq0.1 sq1.1 sb.1 sq3.1 sq2.1 sb.2 sq0.2
+        sq1.2 sq2.2 sq3.2""",
+    "pe": """
+        wf.0 w0B.0 w0A.0 dq1B.0 w1B.0 w1A.0 dq1A.0 dq2B.0 dx1A.0 dq2A.0 dx1B.0 dx2B.0 dx2A.0 wdA.0 wdB.0 xs.0 w0A.1 w0B.1 w1A.1
+        w1B.1 dx11.1 xs.1 rk.1 dx10.1 dx20.1 dq0.1 dx21.1 dq1.1 wf.1 dx12.1 dx13.1 wdA.1 dq3.1 dx23.1 dq2.1 dx22.1 wdB.1 w0A.2
+        w0B.2 w1A.2 w1B.2 dx10.2 dx11.2 dx20.2 dx21.2 dx13.2 dq0.2 dq1.2 rk.2 dx23.2 dx12.2 dq3.2 dx22.2 dq2.2 wdA.2 wdB.2 wf.2
+        xs.2 w0B.3 w0A.3 wn.3 rk.3 w1A.3 nbs.3 w1B.3 dx10.3 dq0.3 dx11.3 dx20.3 dx21.3 dq1.3 wf.3 dq2.3 fs.3 wdA.3 dx12.3
+        dx22.3 dx13.3 dq3.3 dx23.3 wdB.3""",
+    "act": """
+        l_pin l_cu z2 c_wi c_za qA c_z c_ida c_zf c_id c_va g0A.0 g1B.0 nk0A.0 rx.0 x1A.0 x1B.0 ab1A.0 ab1B.0 ab2A.0 ab2B.0
+        c_blka c_blk xa.0 xb.0 g0A.1 g0B.1 nk0A.1 g1A.1 xa.1 x1A.1 x2A.1 x1B.1 nk1A.1 ab0.1 ab1.1 x2B.1 nk1B.1 rx.1 ab3.1 ab2.1
+        xv.1 g0A.2 g0B.2 g1A.2 nk0A.2 g1B.2 x1B.2 x2B.2 ab1.2 nk1B.2 ab0.2 nk1A.2 ab3.2 ab2.2 xa.2 xb.2 xv.2 rx.2 g0B.3 g0A.3
+        x1B.3 g1A.3 g1B.3 ynf.3 x1A.3 x2A.3 ab0.3 ab1.3 x2B.3 ff.3 ab2.3 ab3.3""",
+    "dve": """
+        zfr z0 z1 z3 hi lo c_g c_i pinu c_zc c_if c_m1 c_b fr_t cu4 cuu c_a c_af fr_d c_j th8 g0B.0 c_m0 c_z8 c_idk fu.0 mn.0
+        c_idn c_l2 qB nu0B.0 c_h nk0B.0 a4.0 c_m128 nu0A.0 c_l1 g1A.0 nu1B.0 nk1B.0 x2B.0 nu1A.0 c_gf x2A.0 sa.0 nk1A.0 sf.0
+        kaA.0 kbA.0 anu.0 minA.0 kaB.0 kbB.0 andA.0 minB.0 puA.0 andB.0 sg0.0 sg1.0 c_gt0 puB.0 eqn.0 sg2.0 xv.0 nu0A.1 sg3.0
+        sx.0 nu0B.1 nk0B.1 g1B.1 nu1A.1 eqo.0 xb.1 bit.1 mo.1 nu1B.1 ho.1 rel.1 cum.1 c_fb pos.1 ac.1 posu.1 ad.1 sl0.1 au.1
+        sa.1 fu.1 mn.1 sf.1 kaA.1 kbA.1 minA.1 andA.1 a4.1 puA.1 anu.1 sg0.1 sg1.1 eqo.1 kaB.1 kbB.1 minB.1 andB.1 puB.1 sg3.1
+        sg2.1 nu0A.2 eqn.1 sx.1 nu0B.2 x1A.2 nk0B.2 nu1A.2 vv.1 x2A.2 nu1B.2 bit.2 mo.2 ho.2 rel.2 cum.2 pos.2 ac.2 posu.2 ad.2
+        sl0.2 au.2 sl1.2 kaA.2 kbA.2 sa.2 kaB.2 kbB.2 minA.2 minB.2 fu.2 andB.2 sf.2 puB.2 andA.2 mn.2 a4.2 puA.2 anu.2 sg0.2
+        sg1.2 sx.2 nu0B.3 sg2.2 nk0B.3 eqo.2 nu0A.3 eqn.2 sg3.2 bit.3 mo.3 vv.2 ho.3 rel.3 cum.3 nk0A.3 pos.3 ac.3 posu.3 sl0.3
+        nu1A.3 sl1.3 sl2.3 nbf.3 nu1B.3 ad.3 au.3 nk1B.3 fu.3 nk1A.3 sf.3 kaA.3 kbA.3 minA.3 andA.3 puA.3 sa.3 sg0.3 sg1.3
+        kaB.3 kbB.3 fin0.3 minB.3 fin1.3 andB.3 puB.3 ypf.3 sg3.3 sg2.3 fin3.3 fin2.3""",
+}
 
 
 def plan():
     ops = build_ops()
     deps = find_deps(ops)
-    order, eng = [], [None] * len(ops)
-    for word in ORDER.split():
-        k = int(word.rstrip("a"))
-        able = list(ops[k]["cost"]) or [None]
-        eng[k] = able[0] if len(able) == 1 else ("act" if word.endswith("a") else "dve")
-        assert all(j in order for j in deps[k])
-        order.append(k)
-    assert len(set(order)) == len(ops)
+    number = {o["name"] + ("" if o["p"] == "" else ".%d" % o["p"]): k for k, o in enumerate(ops)}
+    lists = {e: [number[w] for w in text.split()] for e, text in QUEUES.items()}
+    eng, order, done = [None] * len(ops), [], set()
+    while len(order) < len(ops):
+        before = len(order)
+        for e, calls in lists.items():
+            while calls and all(j in done for j in deps[calls[0]]):
+                k = calls.pop(0)
+                eng[k] = e
+                new = [k, k + 1] if ops[k]["kind"] == "send" else [k]
+                order += new
+                done.update(new)
+        assert len(order) > before
+    for k in order:
+        if ops[k].get("group"):
+            mates = [j for j in order if ops[j].get("group") == ops[k]["group"]]
+            ops[k].update({"first": k == mates[0], "last": k == mates[-1]})
     return ops, deps, eng, order
 
 
@@ -417,16 +508,15 @@ PLAN = []
 def ways(T, topo, r):
     src, out = T.cores[r], {}
     for names, dst in ((list(range(NCH)), T.cores[(r + 1) % len(T.cores)]), (["b"], T.cores[r - 1])):
-        if topo.may_write(src, dst):
-            for s in names:
-                out[s] = [src, dst]
-            continue
         able = [c for c in topo.cores_of(src) if T.rank_of(c) is None and topo.may_write(c, dst)]
         near = [c for c in able if topo.die(c) == topo.die(src)]
         far = [c for c in able if c not in near]
-        turn = [c for pair in zip(near, far) for c in pair] or able
-        for k, s in enumerate(names):
-            out[s] = [src, turn[k % len(turn)], dst]
+        if topo.may_write(src, dst):
+            near = [src] * len(far)
+        turn = [c for pair in zip(near, far) for c in pair]
+        for s in names:
+            via = turn[2 if s == "b" else s]
+            out[s] = [src, dst] if via == src else [src, via, dst]
     return out
 
 
@@ -459,7 +549,7 @@ def rank_program(g, core, T, topo):
         return
     n = len(T.cores)
     out = ways(T, topo, rank)
-    X = {s: topo.addr(w[1], core) + (topo.mask(core, w[1]),) for s, w in out.items()}
+    R = {s: topo.addr(w[1], core) + (topo.mask(core, w[1]),) for s, w in out.items()}
     comes = dict(ways(T, topo, (rank - 1) % n))
     comes["b"] = ways(T, topo, (rank + 1) % n)["b"]
     token, total, sent = {}, {}, 0
@@ -489,7 +579,7 @@ def rank_program(g, core, T, topo):
                 queue[e].wait_ge(T.sem[s], v)
                 seen[e][s] = v
                 waited[s] = max(waited.get(s, 0), v)
-        ins = ops[k]["emit"](queue[e], T, e, X)
+        ins = ops[k]["emit"](queue[e], T, e, R)
         if ops[k]["kind"] != "send":
             ins.then_inc(T.sem[token[k][0]], 1 if ops[k]["kind"] == "c" else 16)
     g.wait_ge(T.sem.sent, sent)

@@ -1,3 +1,4 @@
+from concourse.bass import DstId, RemoteDMATransfer
 from concourse.mybir import AluOpType, ActivationFunctionType
 
 ALU, AF = AluOpType, ActivationFunctionType
@@ -8,9 +9,10 @@ BF, F32, I32, U16 = "bfloat16", "float32", "int32", "uint16"
 SCL = [2.0 ** (p - 4) for p in range(PH)]
 QB = [241.0, 177.0, 145.0, 129.0]
 TB = [113.0, 113.0, 113.0, -127.0]
-MODE = ["hop", "chunk", "chunk", "chunk"]
-LAST = [1, 1]
-SILU = [False, False, False]
+MODE = ["hop", "hop", "hop", "hop"]
+XCUT = [0, 768, W]
+LAST = [2, 1]
+SPLIT = [1]
 RND = 1.5 * 2 ** 23
 
 
@@ -23,13 +25,12 @@ SCRATCH = {
     "ths": sb(64, I32), "cus": sb(16, I32), "frs": sb(RG, I32), "frt": sb(RG, BF), "f0": sb(RG, BF),
     "qin": sb(4096, BF), "qout": sb(4096, BF), "bin": sb(192, BF), "kin": sb(192, I32), "thn": sb(64, F32),
     "pu": sb([10, 80], U16), "pw": sb([10, 64], I32), "km": sb([8, 64], I32), "key": sb([4, 2, 32], F32),
-    "n1u": sb(320, U16), "n2u": sb(256, U16), "nk": sb([4, 2, 80], F32), "jc": sb(64, F32),
+    "n1u": sb(320, U16), "n2u": sb(320, U16), "nk": sb([4, 2, 80], F32), "jc": sb(64, F32),
     "g0": sb(4 * 1216, BF), "g1": sb(1216, BF), "xh": sb(8 * HF, BF), "ab": sb([2, 1024], BF), "ss": sb(1024, BF),
     "th8": sb(64, F32), "xab": sb(2 * RG, BF), "xv": sb(RG, BF), "m128": sb(RG, BF),
     "fu": sb(64, U16), "au": sb(64, U16), "a4": sb(64, F32), "mx": sb(16, F32), "mn": sb(16, F32), "valid": sb(48, F32),
     "retx": sb(144, F32), "hm": sb(4 * 288, BF), "ho": sb(288, BF), "rel": sb(36, BF), "cum": sb(36, BF),
     "pos": sb(36, F32), "posu": sb(36, U16), "fb": sb(2048 + 3 * RG, BF), "ff": sb(2 * RG, F32),
-    "fw": sb(2048 + 3 * RG, F32), "fs": sb(3 * RG, F32),
     "ci": sb(8, I32), "cf": sb(16, F32), "wi": sb(12, F32), "ioy": sb(144, F32), "iog": sb(128, F32), "iol": sb(16, F32),
     "ioj": sb(64, F32), "iow": sb(3 * RG, BF), "keep": sb(288, BF), "ee": sb(36, F32),
     "zz": sb(144, BF), "z8": sb(144, BF), "zf": sb(144, BF), "id1": sb(128, BF), "idn": sb(128, BF), "idk": sb(128, BF),
@@ -38,7 +39,7 @@ SCRATCH = {
 }
 SCRATCH.update({b: ("psum", [128, 512], F32) for b in ("d0", "d1", "d2", "d3", "wa", "wb", "wr", "ws")})
 LOADS = ["nx", "x0", "x1", "x2", "x3", "hi", "lo", "pin", "cu", "th", "fr0", "fr1", "q", "yq0", "yq1", "yq2", "yq3", "yp", "yn", "mf"]
-SEMAPHORES = (["dve", "act", "pe", "pool", "sent", "th"] + ["l_" + s for s in LOADS]
+SEMAPHORES = (["dve", "act", "pe", "pool", "sent"] + ["th%d" % c for c in range(NCH)] + ["l_" + s for s in LOADS]
               + ["q%d_%d" % (p, c) for p in range(PH - 1) for c in range(NCH)] + ["b%d" % p for p in range(PH - 1)])
 
 CY, PCY, GA, SC = 0.00104, 0.00052, 1.55, 3.8
@@ -191,12 +192,14 @@ def build_ops():
     def store(sem, eng, dst, in_):
         add("l_" + sem, {eng: 0.06}, lambda q, T, e, R: q.dma_start(dst(T), ap(T, in_)), [in_], [], "dma", "l_" + sem)
 
-    def send(name, sem, way, out, in_):
+    def send(name, pieces):
         def emit(q, T, e, R):
-            rid, pid, mask = R[way]
-            q.remote_dma(ap(T, out), ap(T, in_), T.sem[sem], T.sem.sent, pid, rid, mask)
-        k = add(name, {"pool": 0.3}, emit, [in_], [], "send")
-        add("r" + name, {}, way, [], [out], "recv", sem, k)
+            to = R([way for sem, way, out, in_ in pieces])
+            q.remote_dma_fused([RemoteDMATransfer(dst_ids=[DstId(rid=rid, pnc=pid)], dma_engine_mask=mask, remote_sem=T.sem[sem],
+                                                  src=ap(T, in_), dst=ap(T, out))
+                                for (sem, way, out, in_), (rid, pid, mask) in zip(pieces, to)], local_sem=T.sem.sent)
+        k = add(name, {"pool": 1.0}, emit, [x[3] for x in pieces], [], "send")
+        add("r" + name, {}, pieces, [], [x[2] for x in pieces], "recv", None, k)
 
     def rows(buf, r, c1):
         return X(buf, slice(0, c1), rows=slice(r, 128, 16))
@@ -214,14 +217,14 @@ def build_ops():
     id1, idn, blk = A("id1", 0, 128), A("idn", 0, 128), A("blk", 0, 128)
     hi, lo = A("dg", 0, 256), A("dg", 256, 512)
     load("nx", "sp", A("nxs", 0, 256), lambda T: T.nx[:])
-    load("pin", "act", X("pw", 0, ALL), lambda T: T.pin[:])
-    load("cu", "act", A("cus", 0, 16), lambda T: T.cu[:])
-    for k in range(4):
-        load("x%d" % k, "sp", A("xt", k * W // 4, (k + 1) * W // 4), lambda T, k=k: T.x[:, k * W // 4:(k + 1) * W // 4])
-    memset("z0", A("mt", 0, W // 4), 0.0)
-    memset("z1", A("mt", W // 4, W // 2), 0.0)
-    for k in (2, 3):
-        lin("z%d" % k, A("mt", k * W // 4, (k + 1) * W // 4), A("mt", 0, W // 4), 1.0, 0.0)
+    load("pin", "sp", X("pw", 0, ALL), lambda T: T.pin[:])
+    load("cu", "sp", A("cus", 0, 16), lambda T: T.cu[:])
+    for k, (c0, c1) in enumerate(zip(XCUT, XCUT[1:])):
+        load("x%d" % k, "sp", A("xt", c0, c1), lambda T, c0=c0, c1=c1: T.x[:, c0:c1])
+    memset("z0", A("mt", 0, HF), 0.0)
+    memset("z1", A("mt", HF, 3 * HF), 0.0)
+    for k in range(3, 8):
+        lin("z%d" % k, A("mt", k * HF, (k + 1) * HF), A("mt", 0, HF), 1.0, 0.0)
     cp("hi", hi, A("nxs", 0, 256))
     tt("lo", lo, A("nxs", 0, 256), hi, ALU.subtract)
     move("hi", "sp", rows("mt", 0, W), hi)
@@ -247,11 +250,7 @@ def build_ops():
     lin("c_zf", A("zf", 0, 144), A("zz", 0, 144), 1.0 / W, 0.0)
     same("c_id", id1, A("ioy", 0, 128), col("cf", 0))
     lin("c_idn", idn, id1, -1.0, 0.0)
-    if any(SILU):
-        act("c_idk", A("idk", 0, 128), id1, AF.Silu, 2048.0, 0.0)
-        ops[-1]["cost"]["act"] += 1.3
-    else:
-        lin("c_idk", A("idk", 0, 128), id1, 2048.0, 0.0)
+    lin("c_idk", A("idk", 0, 128), id1, 2048.0, 0.0)
     ts("c_i", col("ci", 4), col("ci", 0), 15, ALU.bitwise_and)
     cp("c_if", col("cf", 9), col("ci", 4))
     lin("c_j", A("jc", 0, 64), A("ioj", 0, 64), 1.0, col("cf", 9))
@@ -270,16 +269,11 @@ def build_ops():
     add("c_gtn", {"pool": 0.21 + 256 * CY},
         lambda q, T, e, R: q.affine_select(T.gtn[:], T.gt0[:], [[-1, 128]], ALU.is_gt, 0.0, 0, 1), [A("gt0", 0, 128)], [A("gtn", 0, 128)])
     lin("c_fb", A("fb", 2048, 2048 + 3 * RG), A("iow", 0, 3 * RG), col("cf", 6), col("cf", 7))
-    for p in range(PH - 1):
-        if SILU[p]:
-            lin("c_fw%d" % p, A("fw", 2048 + RG * p, 2048 + RG * p + RG), A("fb", 2048, 2048 + RG), 1.0, 64.0)
-    lin("c_m128", A("m128", 0, RG), A("mt", 0, RG), 0.0, -128.0)
-    lin("c_va", A("valid", 0, 12), A("ioy", 0, 12), 0.0, 1.0)
+    lin("c_m128", A("m128", 0, RG), A("iow", 0, RG), 0.0, -128.0)
     cp("pinu", pu(0, 12, 76), X("pw", 0, ALL))
     cp("cuu", pu(0, 0, 12), A("cus", 0, 12))
-    ts("cu4", A("a4", 0, 12), A("cus", 0, 12), 1.0 / W, ALU.mult, 1.0, ALU.add)
     ts("th8", A("th8", 0, 64), A("ths", 0, 64), 8192.0, ALU.mult)
-    send("st", "th", "b", A("thn", 0, 64), A("th8", 0, 64))
+    send("st", [("th%d" % c, ("t", c), A("thn", 16 * c, 16 * c + 16), A("th8", 16 * c, 16 * c + 16)) for c in range(NCH)])
     ts("fr_t", A("frt", 0, RG), A("frs", 0, RG), col("cf", 6), ALU.mult)
     tt("fr_d", A("f0", 0, RG), A("frs", 0, RG), A("frt", 0, RG), ALU.subtract)
     for h, H in enumerate("AB"):
@@ -293,28 +287,26 @@ def build_ops():
             A("hm", 288 * p, 288 * p + n8, 2), ALU.mult)
         scan("ho", A("ho", 0, n8), A("keep", 0, n8), A("hm", 288 * K, 288 * K + n8), ALU.mult, ALU.max)
         rel, cum = A("rel", 0, n1), A("cum", 0, n1)
-        tt("rel", rel, A("valid", 0, n1), A("ho", 7, n8, 8), ALU.is_gt)
+        if p:
+            tt("rel", rel, A("valid", 0, n1), A("ho", 7, n8, 8), ALU.is_gt)
+        else:
+            ts("rel", rel, A("ho", 7, n8, 8), 0.5, ALU.is_lt)
         scan("cum", cum, rel, rel, ALU.add, ALU.max)
         mm("rk", [(A("ws", 0, n1), A("gtn", 0, 128), rel), (A("ws", 0, n1), A("idk", 0, 128), rel),
                   (A("ws", 0, n1), blk, cum), (A("ws", 40, 41), blk, A("cum", n1 - 1, n1))])
         tt("pos", A("pos", 0, n1), A("ws", 0, n1), A("ee", 0, n1), ALU.max)
         ts("posu", A("posu", 0, n1), A("pos", 0, n1), -1.0, ALU.add)
-        if p < PH - 2:
+        if p == 0:
+            lin("vv", A("valid", 0, n1), rel, -1.0, 1.0)
+        elif p < PH - 2:
             tt("vv", A("valid", 0, n1), A("valid", 0, n1), rel, ALU.subtract)
         va = A("valid", n1, n1 + 12)
         ts("ac", va, A("wi", 0, 12), A("ws", 40, 41), ALU.is_lt)
         tt("ad", A("mx", 0, 12), A("a4", 16 * K, 16 * K + 12), va, ALU.subtract)
         ts("au", A("au", 16 * K, 16 * K + 12), A("mx", 0, 12), float(W), ALU.mult)
         for k in range(K):
-            off = A("posu", 12 * k, 12 * k + 12)
-            if not SILU[p]:
-                scatter("sl%d" % k, A("fb", RG * p, RG * p + 2048 + RG), off, A("g0", 1216 * k, 1216 * k + RG))
-                continue
-            win, src = A("fw", RG * p, RG * p + 2048 + RG), A("fs", RG * k, RG * k + RG)
-            add("sl%d" % k, {"act": 0.05 + SC * RG * CY},
-                lambda q, T, e, R, win=win, off=off, src=src: q.activation(ind(T, win, off), ap(T, src), AF.Silu), [off, src], [win])
-        if SILU[p]:
-            ts("fr", A("fb", 2048 + RG * p, 2048 + RG * K), A("fw", 2048 + RG * p, 2048 + RG * K), RND, ALU.add, RND + 64.0, ALU.subtract)
+            scatter("sl%d" % k, A("fb", RG * p, RG * p + 2048 + RG), A("posu", 12 * k, 12 * k + 12),
+                    A("g0", 1216 * k, 1216 * k + RG))
 
     for p in range(PH):
         now[0] = p
@@ -325,26 +317,27 @@ def build_ops():
         if p == 0:
             au = pu(0, 0, 12)
         XH = [2 * HF * (h + 2 * (p % 2)) for h in range(2)]
+        g1, G1 = ("g0", 1216) if p == 0 else ("g1", 0)
+        n2, N2 = ("n1u", 80) if p == 0 else ("n2u", 80 * p)
         for h, H in enumerate("AB"):
             bank, k0, k1 = ("wa", 0, 44) if h == 0 else ("wb", 44, 76)
-            n1u, n2u = A("n1u", 80 * p + k0, 80 * p + k1), A("n2u", 64 * p + 32 * h, 64 * p + 32 * h + 32)
-            gather("g0" + H, A("g0", G + 16 * k0, G + 16 * k1), mw, pu(2 * p, k0, k1))
-            wrap("w0" + H, bank, "zz", "g0", G + 16 * k0, G + 16 * k1)
-            cp("nu0" + H, n1u, A(bank, 0, k1 - k0))
-            lin("nk0" + H, nk(p, 0, k0, k1), A(bank, 0, k1 - k0), 1.0, 0.0)
-            gather("g1" + H, A("g1", 16 * k0, 16 * k1), mw, n1u)
-            wrap("w1" + H, bank, "zz", "g1", 16 * (k1 - 32), 16 * k1)
-            cp("nu1" + H, n2u, A(bank, 0, 32))
-            lin("nk1" + H, nk(p, 1, k1 - 32, k1), A(bank, 0, 32), 1.0, float(W))
+            ka, kb = max(k0, 12) if p == 1 else k0, max(k0, 12) if p else k0
+            gather("g0" + H, A("g0", G + 16 * ka, G + 16 * k1), mw, pu(2 * p, ka, k1))
+            wrap("w0" + H, bank, "zz", "g0", G + 16 * ka, G + 16 * k1)
+            cp("nu0" + H, A("n1u", 80 * p + ka, 80 * p + k1), A(bank, 0, k1 - ka))
+            lin("nk0" + H, nk(p, 0, ka, k1), A(bank, 0, k1 - ka), 1.0, 0.0)
+            gather("g1" + H, A(g1, G1 + 16 * k0, G1 + 16 * k1), mw, A("n1u", 80 * p + k0, 80 * p + k1))
+            wrap("w1" + H, bank, "zz", g1, G1 + 16 * kb, G1 + 16 * k1)
+            cp("nu1" + H, A(n2, N2 + kb, N2 + k1), A(bank, 0, k1 - kb))
+            lin("nk1" + H, nk(p, 1, kb, k1), A(bank, 0, k1 - kb), 1.0, float(W))
             gather("x1" + H, A("xh", XH[h], XH[h] + HF), xw, A("n1u", 80 * p + k1 - 32, 80 * p + k1), s, s * (TB[p] - 0.5))
-            gather("x2" + H, A("xh", XH[h] + HF, XH[h] + 2 * HF), xw, n2u, s, s * (TB[p] - 0.5))
-        if any(SILU[p:]):
-            lin("s32", A("fs", RG * p, RG * p + RG), A("g0", G, G + RG), 1.0, 64.0)
+            gather("x2" + H, A("xh", XH[h] + HF, XH[h] + 2 * HF), xw, A(n2, N2 + k1 - 32, N2 + k1), s, s * (TB[p] - 0.5))
         if not last:
-            gather("xa", A("xab", 0, RG), xw, pu(2 * p, 0, 12))
+            if p != 1:
+                gather("xa", A("xab", 0, RG), xw, pu(2 * p, 0, 12))
             gather("xb", A("xab", RG, 2 * RG), xw, A("n1u", 80 * p, 80 * p + 12))
-            mm("xs", [(r0, id1, A("xab", 0, RG)), (r0, id1, A("xab", RG, 2 * RG))])
-            lin("xv", A("xv", 0, RG), r0, 0.5, 127.75)
+            mm("xs", [(r0, id1, A("xv" if p == 1 else "xab", 0, RG)), (r0, id1, A("xab", RG, 2 * RG))])
+            lin("xv", A("xv", 0, RG), r0, 0.5, 63.75 if p == 1 else 127.75)
         else:
             o = A("wr", 0, 256)
             mm("wn", [(o, A("zz", 15 - i, 143 - i), A("mt", 256 * i, 256 * i + 256)) for i in range(16)])
@@ -358,12 +351,15 @@ def build_ops():
         wrap("wf", "ws", "zf", free[0], free[2][0][0], free[2][0][1])
         ts("fu", fu, fw, float(W), ALU.mult)
         if not last:
-            tt("mn", A("mn", 0, 12), fw, a4, ALU.min)
             a4n = A("a4", 16 * p + 16, 16 * p + 28)
-            tt("a4", a4n, A("mn", 0, 12), A("valid", 12 * p, 12 * p + 12), ALU.add)
-            ts("anu", pu(2 * p + 2, 0, 12), a4n, -1.0, ALU.add, float(W), ALU.mult)
+            if p:
+                tt("mn", A("mn", 0, 12), fw, a4, ALU.min)
+                tt("a4", a4n, A("mn", 0, 12), A("valid", 12 * p, 12 * p + 12), ALU.add)
+                ts("anu", pu(2 * p + 2, 0, 12), a4n, -1.0, ALU.add, float(W), ALU.mult)
+            else:
+                lin("a4", a4n, fw, 1.0, 1.0)
             scatter("sa", A("mt", 0, TW), au, free)
-            scatter("sf", A("mt", 0, TW), fu, A("g1", 0, RG))
+            scatter("sf", A("mt", 0, TW), fu, A(g1, G1, G1 + RG))
             scatter("sx", A("xt", 0, TW), fu, A("xv", 0, RG), A("m128", 0, RG))
         else:
             mm("fs", [(r0, blk, free)])
@@ -398,21 +394,32 @@ def build_ops():
             ts("and" + H, pw, km, W - 1, ALU.bitwise_and)
             cp("pu" + H, X("pu", slice(2 * p + 2, 2 * p + 4), slice(32 * h + 12, 32 * h + 44)), pw)
             if h == 1 and not last:
-                send("sb", "b%d" % p, "b", A("kin", 64 * p, 64 * p + 64), X("km", 2 * p, ALL))
-            step = LAST[h] if last else 1
+                send("sb", [("b%d" % p, "b", A("kin", 64 * p, 64 * p + 64), X("km", 2 * p, ALL))])
+            step = LAST[h] if last else 2
             for c in range(2 * h, 2 * h + 2, step):
                 q0, q1 = 1024 * p + CH * c, 1024 * p + CH * (c + step)
                 out = A("ss", CH * c, CH * (c + step)) if last else A("qout", q0, q1)
+                if last and h == 0 and SPLIT[0]:
+                    o = A("d%d" % c, 0, CH * step)
+                    gather("sg%d" % c, out, A("xh", b, b + 2 * HF), pu(2 * p + 3, 12 + 16 * c, 12 + 16 * (c + step)))
+                    mm("sm%d" % c, [(o, id1, A("qin", q0, q1)), (o, id1, out)])
+                    ts("fin%d" % c, A("qout", q0, q1), o, RND, ALU.add, RND + 1.0, ALU.subtract)
+                    store("yq%d" % c, "sp", lambda T, c=c, step=step: T.yq[:, CH * c:CH * (c + step)], A("qout", q0, q1))
+                    continue
                 gtt("sg%d" % c, out, A("xh", b, b + 2 * HF), pu(2 * p + 3, 12 + 16 * c, 12 + 16 * (c + step)), A("qin", q0, q1), ALU.add)
                 if last:
                     ts("fin%d" % c, A("qout", q0, q1), out, RND, ALU.add, RND + 1.0, ALU.subtract)
                     store("yq%d" % c, "sp", lambda T, c=c, step=step: T.yq[:, CH * c:CH * (c + step)], A("qout", q0, q1))
                 else:
-                    send("sq%d" % c, "q%d_%d" % (p, c), c, A("qin", q0 + 1024, q1 + 1024), A("qout", q0, q1))
+                    send("sq" + H, [("q%d_%d" % (p, c + u), c + u, A("qin", q0 + 1024 + CH * u, q0 + 1024 + CH * u + CH),
+                                     A("qout", q0 + CH * u, q0 + CH * u + CH)) for u in range(2)])
         if last:
             break
         K = p + 1
-        gather("rx", A("retx", 48 * p, 48 * K), nk(p, 0, 0, 12), A("l2", 0, 3))
+        if p == 1:
+            gather("rx", A("retx", 48, 96), nk(0, 1, 0, 12), A("l2", 0, 3), 1.0, -float(W))
+        else:
+            gather("rx", A("retx", 48 * p, 48 * K), nk(p, 0, 0, 12), A("l2", 0, 3))
         gtt("eqo", A("hm", 384 * p, 384 * p + 96, 2), X("pw", 2 * p, ALL), A("l1", 0, 3), A("retx", 48 * p, 48 * K), ALU.is_equal)
         gtt("eqn", A("hm", 288 * K, 384 * K, 2), X("pw", 2 * p + 2, ALL), A("l1", 0, 3 * K), A("retx", 0, 48 * K), ALU.is_equal)
     cp("ypf", A("ypf", 0, 64), X("pw", 8, ALL))
@@ -450,32 +457,30 @@ def find_deps(ops):
 
 QUEUES = {
     "sp": """
-        l_nx l_q l_fr1 l_th l_fr0 l_x1 l_hi l_lo l_x0 l_x3 l_x2 l_mf.3 l_yn.3 l_yp.3 l_yq0.3 l_yq1.3 l_yq3.3 l_yq2.3""",
+        l_nx l_q l_th l_fr1 l_fr0 l_cu l_pin l_hi l_lo l_x0 l_x1 l_mf.3 l_yn.3 l_yp.3 l_yq3.3 l_yq0.3 l_yq2.3""",
     "pool": """
-        i_j i_pf i_p i_k i_g i_l i_y i_w st sb.0 sq0.0 sq1.0 sq2.0 sq3.0 c_gtn i_e sq0.1 sq1.1 sb.1 sq3.1 sq2.1 sb.2 sq0.2
-        sq1.2 sq2.2 sq3.2""",
+        i_p i_y i_pf i_l i_j i_w i_e i_g st i_k sb.0 sqA.0 sqB.0 c_gtn sb.1 sqA.1 sqB.1 sb.2 sqA.2 sqB.2""",
     "pe": """
-        wf.0 w0B.0 w0A.0 dq1B.0 w1B.0 w1A.0 dq1A.0 dq2B.0 dx1A.0 dq2A.0 dx1B.0 dx2B.0 dx2A.0 wdA.0 wdB.0 xs.0 w0A.1 w0B.1 w1A.1
-        w1B.1 dx11.1 xs.1 rk.1 dx10.1 dx20.1 dq0.1 dx21.1 dq1.1 wf.1 dx12.1 dx13.1 wdA.1 dq3.1 dx23.1 dq2.1 dx22.1 wdB.1 w0A.2
-        w0B.2 w1A.2 w1B.2 dx10.2 dx11.2 dx20.2 dx21.2 dx13.2 dq0.2 dq1.2 rk.2 dx23.2 dx12.2 dq3.2 dx22.2 dq2.2 wdA.2 wdB.2 wf.2
-        xs.2 w0B.3 w0A.3 wn.3 rk.3 w1A.3 nbs.3 w1B.3 dx10.3 dq0.3 dx11.3 dx20.3 dx21.3 dq1.3 wf.3 dq2.3 fs.3 wdA.3 dx12.3
-        dx22.3 dx13.3 dq3.3 dx23.3 wdB.3""",
+        wf.0 w0B.0 w0A.0 dq2B.0 dq1B.0 w1B.0 w1A.0 dx1B.0 dq1A.0 dx2B.0 dq2A.0 dx1A.0 dx2A.0 wdB.0 wdA.0 xs.0 w0A.1 w0B.1 w1A.1
+        dx1B.1 w1B.1 rk.1 dx1A.1 dx2A.1 dq1A.1 dq2A.1 wf.1 dq1B.1 dq2B.1 dx2B.1 wdA.1 wdB.1 xs.1 w0A.2 w0B.2 w1A.2 w1B.2 dx1A.2
+        rk.2 dx1B.2 xs.2 dq1A.2 dx2A.2 dq2A.2 dx2B.2 dq2B.2 dq1B.2 wf.2 wdA.2 wdB.2 wn.3 w0A.3 w0B.3 w1A.3 nbs.3 w1B.3 rk.3
+        dx1A.3 dx1B.3 dx2A.3 dq2A.3 dq1A.3 dx2B.3 dq1B.3 dq2B.3 wdA.3 wf.3 fs.3 wdB.3 sm0.3""",
     "act": """
-        l_pin l_cu z2 c_wi c_za qA c_z c_ida c_zf c_id c_va g0A.0 g1B.0 nk0A.0 rx.0 x1A.0 x1B.0 ab1A.0 ab1B.0 ab2A.0 ab2B.0
-        c_blka c_blk xa.0 xb.0 g0A.1 g0B.1 nk0A.1 g1A.1 xa.1 x1A.1 x2A.1 x1B.1 nk1A.1 ab0.1 ab1.1 x2B.1 nk1B.1 rx.1 ab3.1 ab2.1
-        xv.1 g0A.2 g0B.2 g1A.2 nk0A.2 g1B.2 x1B.2 x2B.2 ab1.2 nk1B.2 ab0.2 nk1A.2 ab3.2 ab2.2 xa.2 xb.2 xv.2 rx.2 g0B.3 g0A.3
-        x1B.3 g1A.3 g1B.3 ynf.3 x1A.3 x2A.3 ab0.3 ab1.3 x2B.3 ff.3 ab2.3 ab3.3""",
+        z5 z6 z3 qB c_za c_z c_ida c_zf c_id g0B.0 qA g1B.0 nk0B.0 rx.0 x1B.0 x1A.0 ab1B.0 ab2B.0 ab1A.0 ab2A.0 xa.0 xb.0
+        c_blka c_blk xv.0 g0A.1 g0B.1 g1A.1 g1B.1 x1A.1 x2A.1 x2B.1 ab1A.1 ab2A.1 ab1B.1 ab2B.1 xb.1 g0A.2 xv.1 vv.1 g0B.2
+        g1A.2 x1A.2 x1B.2 x2A.2 x2B.2 ab1A.2 ab2A.2 ab2B.2 ab1B.2 xv.2 rx.2 g0A.3 g0B.3 g1A.3 x1A.3 x1B.3 x2A.3 x2B.3 ab2A.3
+        ab1A.3 ab1B.3 ab2B.3 ff.3 sg0.3""",
     "dve": """
-        zfr z0 z1 z3 hi lo c_g c_i pinu c_zc c_if c_m1 c_b fr_t cu4 cuu c_a c_af fr_d c_j th8 g0B.0 c_m0 c_z8 c_idk fu.0 mn.0
-        c_idn c_l2 qB nu0B.0 c_h nk0B.0 a4.0 c_m128 nu0A.0 c_l1 g1A.0 nu1B.0 nk1B.0 x2B.0 nu1A.0 c_gf x2A.0 sa.0 nk1A.0 sf.0
-        kaA.0 kbA.0 anu.0 minA.0 kaB.0 kbB.0 andA.0 minB.0 puA.0 andB.0 sg0.0 sg1.0 c_gt0 puB.0 eqn.0 sg2.0 xv.0 nu0A.1 sg3.0
-        sx.0 nu0B.1 nk0B.1 g1B.1 nu1A.1 eqo.0 xb.1 bit.1 mo.1 nu1B.1 ho.1 rel.1 cum.1 c_fb pos.1 ac.1 posu.1 ad.1 sl0.1 au.1
-        sa.1 fu.1 mn.1 sf.1 kaA.1 kbA.1 minA.1 andA.1 a4.1 puA.1 anu.1 sg0.1 sg1.1 eqo.1 kaB.1 kbB.1 minB.1 andB.1 puB.1 sg3.1
-        sg2.1 nu0A.2 eqn.1 sx.1 nu0B.2 x1A.2 nk0B.2 nu1A.2 vv.1 x2A.2 nu1B.2 bit.2 mo.2 ho.2 rel.2 cum.2 pos.2 ac.2 posu.2 ad.2
-        sl0.2 au.2 sl1.2 kaA.2 kbA.2 sa.2 kaB.2 kbB.2 minA.2 minB.2 fu.2 andB.2 sf.2 puB.2 andA.2 mn.2 a4.2 puA.2 anu.2 sg0.2
-        sg1.2 sx.2 nu0B.3 sg2.2 nk0B.3 eqo.2 nu0A.3 eqn.2 sg3.2 bit.3 mo.3 vv.2 ho.3 rel.3 cum.3 nk0A.3 pos.3 ac.3 posu.3 sl0.3
-        nu1A.3 sl1.3 sl2.3 nbf.3 nu1B.3 ad.3 au.3 nk1B.3 fu.3 nk1A.3 sf.3 kaA.3 kbA.3 minA.3 andA.3 puA.3 sa.3 sg0.3 sg1.3
-        kaB.3 kbB.3 fin0.3 minB.3 fin1.3 andB.3 puB.3 ypf.3 sg3.3 sg2.3 fin3.3 fin2.3""",
+        z0 zfr z7 z1 z4 hi lo c_g th8 c_zc c_i c_a c_gf c_m1 pinu c_af c_m128 c_b c_l2 fr_t cuu fr_d c_idn g0A.0 c_z8 nu0B.0
+        c_h c_if fu.0 c_wi nu0A.0 nk0A.0 g1A.0 c_m0 nu1B.0 c_j x2B.0 nu1A.0 nk1B.0 c_l1 x2A.0 sa.0 nk1A.0 sf.0 kaB.0 kbB.0
+        kaA.0 kbA.0 minB.0 minA.0 andA.0 andB.0 puA.0 puB.0 sg0.0 sg2.0 nu0A.1 sx.0 nu0B.1 nk0A.1 eqo.0 x1B.1 c_idk a4.0 eqn.0
+        nk0B.1 bit.1 c_gt0 nu1A.1 mo.1 rx.1 ho.1 rel.1 nu1B.1 cum.1 c_fb nk1B.1 pos.1 ac.1 posu.1 ad.1 sl0.1 au.1 sa.1 nk1A.1
+        fu.1 eqo.1 sf.1 kaA.1 kbA.1 mn.1 minA.1 a4.1 andA.1 anu.1 puA.1 kaB.1 kbB.1 minB.1 sg0.1 andB.1 puB.1 sg2.1 nu0A.2
+        eqn.1 sx.1 nu0B.2 nk0B.2 nk0A.2 g1B.2 xa.2 bit.2 nu1A.2 mo.2 nu1B.2 ho.2 nk1A.2 rel.2 cum.2 xb.2 pos.2 ac.2 posu.2 ad.2
+        sl0.2 au.2 sl1.2 nk1B.2 sa.2 fu.2 mn.2 sf.2 kaA.2 kbA.2 kaB.2 kbB.2 minA.2 minB.2 a4.2 andA.2 anu.2 puA.2 andB.2 sg0.2
+        puB.2 eqo.2 sg2.2 nu0A.3 nk0A.3 sx.2 nu0B.3 vv.2 ynf.3 eqn.2 g1B.3 bit.3 nk0B.3 mo.3 nu1A.3 ho.3 rel.3 cum.3 nu1B.3
+        nbf.3 pos.3 ac.3 posu.3 nk1A.3 sl0.3 sl1.3 ad.3 sl2.3 au.3 kaA.3 kbA.3 minA.3 nk1B.3 andA.3 fu.3 puA.3 sf.3 kaB.3 kbB.3
+        sa.3 minB.3 andB.3 puB.3 ypf.3 sg3.3 fin3.3 fin0.3 sg2.3 fin2.3""",
 }
 
 
@@ -506,18 +511,25 @@ PLAN = []
 
 
 def ways(T, topo, r):
-    src, out = T.cores[r], {}
-    for names, dst in ((list(range(NCH)), T.cores[(r + 1) % len(T.cores)]), (["b"], T.cores[r - 1])):
-        able = [c for c in topo.cores_of(src) if T.rank_of(c) is None and topo.may_write(c, dst)]
-        near = [c for c in able if topo.die(c) == topo.die(src)]
-        far = [c for c in able if c not in near]
-        if topo.may_write(src, dst):
-            near = [src] * len(far)
-        turn = [c for pair in zip(near, far) for c in pair]
-        for s in names:
-            via = turn[2 if s == "b" else s]
-            out[s] = [src, dst] if via == src else [src, via, dst]
+    src, nxt, prv = T.cores[r], T.cores[(r + 1) % len(T.cores)], T.cores[r - 1]
+    able = [c for c in topo.cores_of(src) if T.rank_of(c) is None and topo.may_write(c, nxt) and topo.may_write(c, prv)]
+    near = [c for c in able if topo.die(c) == topo.die(src)]
+    far = [c for c in able if c not in near]
+    lane = [c for pair in zip(near, far) for c in pair]
+    out = {"b": [src, prv] if topo.may_write(src, prv) else [src, lane[2], prv]}
+    for c in range(NCH):
+        out[c] = [src, nxt] if lane[c] in near and topo.may_write(src, nxt) else [src, lane[c], nxt]
+        out["t", c] = [src, lane[c], prv]
     return out
+
+
+def shares(topo, paths):
+    allowed = [topo.engines(w[0], w[1]) for w in paths]
+    most, taken, out = max(len(a) for a in allowed) // len(paths), [], {}
+    for k in sorted(range(len(paths)), key=lambda k: len(allowed[k])):
+        out[k] = [e for e in allowed[k] if e not in taken][:most]
+        taken += out[k]
+    return [out[k] for k in range(len(paths))]
 
 
 def relay_program(g, core, T, topo, ops, order):
@@ -525,16 +537,16 @@ def relay_program(g, core, T, topo, ops, order):
     for r in [r for r, c in enumerate(T.cores) if core in topo.cores_of(c)]:
         way = ways(T, topo, r)
         for k in order:
-            if ops[k]["kind"] != "send":
+            if ops[k]["kind"] != "recv":
                 continue
-            o = ops[k + 1]
-            if len(way[o["emit"]]) == 3 and way[o["emit"]][1] == core:
-                src, me, dst = way[o["emit"]]
-                piece = T[o["w"][0][0]][o["w"][0][1]]
-                rid, pid = topo.addr(dst, core)
-                g.wait_ge(T.sem[o["sem"]], len(topo.engines(src, core)))
-                g.remote_dma(piece, piece, T.sem[o["sem"]], T.sem.sent, pid, rid, topo.mask(core, dst))
-                sent += len(topo.engines(core, dst))
+            paths = [way[x[1]] for x in ops[k]["emit"]]
+            for (sem, name, place, source), path, used in zip(ops[k]["emit"], paths, shares(topo, paths)):
+                if len(path) == 3 and path[1] == core:
+                    piece = T[place[0]][place[1]]
+                    rid, pid = topo.addr(path[2], core)
+                    g.wait_ge(T.sem[sem], len(used))
+                    g.remote_dma(piece, piece, T.sem[sem], T.sem.sent, pid, rid, topo.mask(core, path[2]))
+                    sent += len(topo.engines(core, path[2]))
     if sent:
         g.wait_ge(T.sem.sent, sent)
 
@@ -549,20 +561,25 @@ def rank_program(g, core, T, topo):
         return
     n = len(T.cores)
     out = ways(T, topo, rank)
-    R = {s: topo.addr(w[1], core) + (topo.mask(core, w[1]),) for s, w in out.items()}
+
+    def R(names):
+        paths = [out[s] for s in names]
+        return [topo.addr(w[1], core) + (sum(1 << e for e in used),) for w, used in zip(paths, shares(topo, paths))]
     comes = dict(ways(T, topo, (rank - 1) % n))
-    comes["b"] = ways(T, topo, (rank + 1) % n)["b"]
+    comes.update({s: w for s, w in ways(T, topo, (rank + 1) % n).items() if s not in range(NCH)})
     token, total, sent = {}, {}, 0
     for k in order:
         o = ops[k]
         if o["kind"] == "c":
             total[eng[k]] = total.get(eng[k], 0) + 1
-            token[k] = (eng[k], total[eng[k]])
+            token[k] = [(eng[k], total[eng[k]])]
         elif o["kind"] == "dma":
-            token[k] = (o["sem"], 16)
+            token[k] = [(o["sem"], 16)]
         elif o["kind"] == "recv":
-            token[k] = (o["sem"], len(topo.engines(comes[o["emit"]][-2], core)))
-            sent += len(topo.engines(core, out[o["emit"]][1]))
+            paths = [comes[x[1]] for x in o["emit"]]
+            token[k] = [(x[0], len(used if len(w) == 2 else topo.engines(w[1], core)))
+                        for x, w, used in zip(o["emit"], paths, shares(topo, paths))]
+            sent += sum(len(used) for used in shares(topo, [out[x[1]] for x in o["emit"]]))
     queue = {"dve": g.vector, "act": g.scalar, "pe": g.tensor, "pool": g, "sp": g.sync}
     waited, seen = {}, {e: {} for e in queue}
     for k in order:
@@ -572,8 +589,8 @@ def rank_program(g, core, T, topo):
         need = {}
         for j, both_read in deps[k].items():
             if not (eng[j] == e and (e == "pe" or both_read)):
-                s, v = token[j]
-                need[s] = max(need.get(s, 0), v)
+                for s, v in token[j]:
+                    need[s] = max(need.get(s, 0), v)
         for s, v in need.items():
             if seen[e].get(s, 0) < v:
                 queue[e].wait_ge(T.sem[s], v)
@@ -581,8 +598,8 @@ def rank_program(g, core, T, topo):
                 waited[s] = max(waited.get(s, 0), v)
         ins = ops[k]["emit"](queue[e], T, e, R)
         if ops[k]["kind"] != "send":
-            ins.then_inc(T.sem[token[k][0]], 1 if ops[k]["kind"] == "c" else 16)
+            ins.then_inc(T.sem[token[k][0][0]], 1 if ops[k]["kind"] == "c" else 16)
     g.wait_ge(T.sem.sent, sent)
-    for s, v in list(total.items()) + [t for k, t in token.items() if ops[k]["kind"] != "c"]:
+    for s, v in list(total.items()) + [t for k in token for t in token[k] if ops[k]["kind"] != "c"]:
         if waited.get(s, 0) < v:
             g.sync.wait_ge(T.sem[s], v)

from concourse.bass import DstId, RemoteDMATransfer
from concourse.mybir import AluOpType, ActivationFunctionType

ALU, AF = AluOpType, ActivationFunctionType
PH, W, RG = 4, 4096, 192
NCH, CH, HF = 4, 256, 512
TW = 2 * W + RG
BF, F32, I32, U16 = "bfloat16", "float32", "int32", "uint16"
SCL = [2.0 ** (p - 4) for p in range(PH)]
QB = [241.0, 177.0, 145.0, 129.0]
TB = [113.0, 113.0, 113.0, -127.0]
MODE = ["hop", "hop", "hop", "hop"]
XCUT = [0, 768, W]
LAST = [2, 1]
SPLIT = [1]
RND = 1.5 * 2 ** 23


def sb(n, dtype):
    return ("sbuf", [128] + (n if isinstance(n, list) else [n]), dtype)


SCRATCH = {
    "xt": sb(TW, BF), "mt": sb(TW, BF), "mf": sb(TW, F32), "nxs": sb(256, I32), "dg": sb(512, BF), "qraw": sb(1024, BF),
    "ths": sb(64, I32), "cus": sb(16, I32), "frs": sb(RG, I32), "frt": sb(RG, BF), "f0": sb(RG, BF),
    "qin": sb(4096, BF), "qout": sb(4096, BF), "bin": sb(192, BF), "kin": sb(192, I32), "thn": sb(64, F32),
    "pu": sb([10, 80], U16), "pw": sb([10, 64], I32), "km": sb([8, 64], I32), "key": sb([4, 2, 32], F32),
    "n1u": sb(320, U16), "n2u": sb(320, U16), "nk": sb([4, 2, 80], F32), "jc": sb(64, F32),
    "g0": sb(4 * 1216, BF), "g1": sb(1216, BF), "xh": sb(8 * HF, BF), "ab": sb([2, 1024], BF), "ss": sb(1024, BF),
    "th8": sb(64, F32), "xab": sb(2 * RG, BF), "xv": sb(RG, BF), "m128": sb(RG, BF),
    "fu": sb(64, U16), "au": sb(64, U16), "a4": sb(64, F32), "mx": sb(16, F32), "mn": sb(16, F32), "valid": sb(48, F32),
    "retx": sb(144, F32), "hm": sb(4 * 288, BF), "ho": sb(288, BF), "rel": sb(36, BF), "cum": sb(36, BF),
    "pos": sb(36, F32), "posu": sb(36, U16), "fb": sb(2048 + 3 * RG, BF), "ff": sb(2 * RG, F32),
    "ci": sb(8, I32), "cf": sb(16, F32), "wi": sb(12, F32), "ioy": sb(144, F32), "iog": sb(128, F32), "iol": sb(16, F32),
    "ioj": sb(64, F32), "iow": sb(3 * RG, BF), "keep": sb(288, BF), "ee": sb(36, F32),
    "zz": sb(144, BF), "z8": sb(144, BF), "zf": sb(144, BF), "id1": sb(128, BF), "idn": sb(128, BF), "idk": sb(128, BF),
    "blk": sb(128, BF), "gt0": sb(128, BF), "gtn": sb(128, BF), "apart": sb(144, F32),
    "l1": sb(10, U16), "l2": sb(4, U16), "ypf": sb(64, F32), "ynf": sb(256, F32),
}
SCRATCH.update({b: ("psum", [128, 512], F32) for b in ("d0", "d1", "d2", "d3", "wa", "wb", "wr", "ws")})
LOADS = ["nx", "x0", "x1", "x2", "x3", "hi", "lo", "pin", "cu", "th", "fr0", "fr1", "q", "yq0", "yq1", "yq2", "yq3", "yp", "yn", "mf"]
SEMAPHORES = (["dve", "act", "pe", "pool", "sent"] + ["th%d" % c for c in range(NCH)] + ["l_" + s for s in LOADS]
              + ["q%d_%d" % (p, c) for p in range(PH - 1) for c in range(NCH)] + ["b%d" % p for p in range(PH - 1)])

CY, PCY, GA, SC = 0.00104, 0.00052, 1.55, 3.8
ALL = slice(None)


def X(buf, *idx, rows=ALL):
    shape = SCRATCH[buf][1][1:]
    starts, n = [0], 1
    for k, size in enumerate(shape):
        i = idx[k]
        r = range(size)[i] if isinstance(i, slice) else range(i, i + 1)
        n *= len(r)
        if k < len(shape) - 1:
            starts = [s * size + v for s in starts for v in r]
        else:
            runs = [(s * size + r[0], s * size + r[-1] + 1) for s in starts]
    return (buf, (rows,) + idx, runs, set(range(128)[rows]), n)


def A(buf, c0, c1, step=1):
    return X(buf, slice(c0, c1, step))


def width(a):
    return a[4]


def two(*aps):
    return all(SCRATCH[a[0]][2] in (BF, U16) for a in aps)


def build_ops():
    ops, now = [], [""]

    def add(name, cost, emit, reads, writes, kind="c", sem=None, after=None):
        ops.append({"name": name, "p": now[0], "cost": cost, "emit": emit, "r": reads, "w": writes, "kind": kind,
                    "sem": sem, "after": after})
        return len(ops) - 1

    def ap(T, a):
        return T[a[0]][a[1]]

    def ind(T, win, off):
        return ap(T, win).indirect(ap(T, off))

    def cyc(n):
        return max(64, n) * CY

    def sc(T, s):
        return ap(T, s) if isinstance(s, tuple) else s

    def ts(name, out, in0, s1, op0, s2=None, op1=None):
        n = width(out)
        cols = [s for s in (s1, s2) if isinstance(s, tuple)]

        def emit(q, T, e, R):
            if op1 is None:
                return q.tensor_scalar(ap(T, out), ap(T, in0), sc(T, s1), None, op0)
            return q.tensor_scalar(ap(T, out), ap(T, in0), sc(T, s1), sc(T, s2), op0, op1)
        add(name, {"dve": cyc(n / 2 if two(out, in0) else n)}, emit, [in0] + cols, [out])

    def tt(name, out, in0, in1, op):
        k = 1 if "psum" in (SCRATCH[in0[0]][0], SCRATCH[in1[0]][0]) else 2
        add(name, {"dve": cyc(k * width(out))}, lambda q, T, e, R: q.tensor_tensor(ap(T, out), ap(T, in0), ap(T, in1), op),
            [in0, in1], [out])

    def cp(name, out, in_):
        n = width(out)
        add(name, {"dve": cyc(n / 2 if two(out, in_) else n)}, lambda q, T, e, R: q.tensor_copy(ap(T, out), ap(T, in_)),
            [in_], [out])

    def affine(q, e, out, in_, scale, bias):
        if e == "act":
            if isinstance(bias, float) and bias == 0.0:
                return q.activation(out, in_, AF.Copy, scale=scale)
            return q.activation(out, in_, AF.Identity, bias=bias, scale=scale)
        return q.tensor_scalar(out, in_, scale, bias, ALU.mult, ALU.add)

    def lin(name, out, in_, scale, bias):
        n = width(in_)
        add(name, {"act": cyc(n), "dve": cyc(n / 2 if two(out, in_) else n)},
            lambda q, T, e, R: affine(q, e, ap(T, out), ap(T, in_), sc(T, scale), sc(T, bias)),
            [in_] + [s for s in (scale, bias) if isinstance(s, tuple)], [out])

    def act(name, out, in_, func, scale, bias):
        add(name, {"act": cyc(width(in_))}, lambda q, T, e, R: q.activation(ap(T, out), ap(T, in_), func, scale=scale, bias=sc(T, bias)),
            [in_] + ([bias] if isinstance(bias, tuple) else []), [out])

    def same(name, out, in_, column):
        apart = A("apart", 0, width(in_))
        act(name + "a", apart, in_, AF.Abs, -1.0, column)
        act(name, out, apart, AF.Relu, -1.0, 1.0)

    def gather(name, out, win, off, scale=None, bias=None):
        n = 16 * width(off)

        def emit(q, T, e, R):
            if scale is not None:
                return affine(q, e, ap(T, out), ind(T, win, off), scale, bias)
            if e == "act":
                return q.activation(ap(T, out), ind(T, win, off), AF.Copy)
            return q.tensor_copy(ap(T, out), ind(T, win, off))
        add(name, {"act": 0.065 + GA * n * CY, "dve": 0.05 + GA * n * CY}, emit, [win, off], [out])

    def gtt(name, out, win, off, in1, op):
        add(name, {"dve": 0.05 + GA * 16 * width(off) * CY},
            lambda q, T, e, R: q.tensor_tensor(ap(T, out), ind(T, win, off), ap(T, in1), op), [win, off, in1], [out])

    def scatter(name, win, off, in_, in1=None):
        def emit(q, T, e, R):
            if in1 is None:
                return q.tensor_copy(ind(T, win, off), ap(T, in_))
            return q.tensor_tensor(ind(T, win, off), ap(T, in_), ap(T, in1), ALU.add)
        add(name, {"dve": 0.05 + SC * 16 * width(off) * CY}, emit, [off, in_] + ([in1] if in1 else []), [win])

    def scan(name, out, d0, d1, op0, op1):
        add(name, {"dve": cyc(width(out) / 2)},
            lambda q, T, e, R: q.tensor_tensor_scan(ap(T, out), ap(T, d0), ap(T, d1), 0.0, op0, op1), [d0, d1], [out])

    def mm(name, parts, group=None):
        def emit(q, T, e, R):
            ins = None
            for k, (o, l, r) in enumerate(parts):
                ins = q.matmul(ap(T, o), ap(T, l), ap(T, r), me["first"] and k == 0, me["last"] and k == len(parts) - 1)
            return ins
        me = ops[add(name, {"pe": sum(max(64, width(o)) for o, l, r in parts) * PCY}, emit,
                     [x for o, l, r in parts for x in (l, r)], [o for o, l, r in parts])]
        me.update({"group": group, "first": True, "last": True})

    def wrap(name, bank, z, buf, c0, c1):
        mm(name, [(A(bank, 0, (c1 - c0) // 16), A(z, 15 - i, 143 - i), A(buf, c0 + i, c1, 16)) for i in range(16)])

    def memset(name, out, v):
        add(name, {"dve": cyc(width(out) / 2 if two(out) else width(out))}, lambda q, T, e, R: q.memset(ap(T, out), v), [], [out])

    def iota(name, out, pat, base, cm):
        def emit(q, T, e, R):
            if SCRATCH[out[0]][2] == I32:
                return q.iota(ap(T, out), pat, base, cm)
            return q.iota(ap(T, out), pat, base, cm, allow_small_or_imprecise_dtypes=True)
        add(name, {"pool": 0.16 + 2 * width(out) * CY}, emit, [], [out])

    def load(sem, eng, out, src, behind=()):
        add("l_" + sem, {eng: 0.06}, lambda q, T, e, R: q.dma_start(ap(T, out), src(T)), list(behind), [out], "dma", "l_" + sem)

    def move(sem, eng, out, in_):
        add("l_" + sem, {eng: 0.06}, lambda q, T, e, R: q.dma_start(ap(T, out), ap(T, in_)), [in_], [out], "dma", "l_" + sem)

    def store(sem, eng, dst, in_):
        add("l_" + sem, {eng: 0.06}, lambda q, T, e, R: q.dma_start(dst(T), ap(T, in_)), [in_], [], "dma", "l_" + sem)

    def send(name, pieces):
        def emit(q, T, e, R):
            to = R([way for sem, way, out, in_ in pieces])
            q.remote_dma_fused([RemoteDMATransfer(dst_ids=[DstId(rid=rid, pnc=pid)], dma_engine_mask=mask, remote_sem=T.sem[sem],
                                                  src=ap(T, in_), dst=ap(T, out))
                                for (sem, way, out, in_), (rid, pid, mask) in zip(pieces, to)], local_sem=T.sem.sent)
        k = add(name, {"pool": 1.0}, emit, [x[3] for x in pieces], [], "send")
        add("r" + name, {}, pieces, [], [x[2] for x in pieces], "recv", None, k)

    def rows(buf, r, c1):
        return X(buf, slice(0, c1), rows=slice(r, 128, 16))

    def col(buf, k):
        return A(buf, k, k + 1)

    def nk(p, hop, k0, k1):
        return X("nk", p, hop, slice(k0, k1))

    def pu(row, k0, k1):
        return X("pu", row, slice(k0, k1))

    xw, mw = A("xt", 0, W), A("mt", 0, W)
    id1, idn, blk = A("id1", 0, 128), A("idn", 0, 128), A("blk", 0, 128)
    hi, lo = A("dg", 0, 256), A("dg", 256, 512)
    load("nx", "sp", A("nxs", 0, 256), lambda T: T.nx[:])
    load("pin", "sp", X("pw", 0, ALL), lambda T: T.pin[:])
    load("cu", "sp", A("cus", 0, 16), lambda T: T.cu[:])
    for k, (c0, c1) in enumerate(zip(XCUT, XCUT[1:])):
        load("x%d" % k, "sp", A("xt", c0, c1), lambda T, c0=c0, c1=c1: T.x[:, c0:c1])
    memset("z0", A("mt", 0, HF), 0.0)
    memset("z1", A("mt", HF, 3 * HF), 0.0)
    for k in range(3, 8):
        lin("z%d" % k, A("mt", k * HF, (k + 1) * HF), A("mt", 0, HF), 1.0, 0.0)
    cp("hi", hi, A("nxs", 0, 256))
    tt("lo", lo, A("nxs", 0, 256), hi, ALU.subtract)
    move("hi", "sp", rows("mt", 0, W), hi)
    move("lo", "sp", rows("mt", 1, W), lo)
    load("q", "sp", A("qraw", 0, 1024), lambda T: T.q[:])
    load("th", "sp", A("ths", 0, 64), lambda T: T.th[:])
    memset("zfr", A("frs", 0, RG), 0)
    for r in range(2):
        load("fr%d" % r, "sp", rows("frs", r, RG), lambda T: T.fr[:])
    iota("i_p", col("ci", 0), [[0, 1]], 0, 1)
    iota("i_pf", col("cf", 0), [[0, 1]], 0, 1)
    iota("i_y", A("ioy", 0, 144), [[1, 144]], 0, 0)
    iota("i_j", A("ioj", 0, 64), [[HF, 2], [16, 32]], 0, 0)
    iota("i_l", A("iol", 0, 9), [[0, 3], [4, 3]], 0, 0)
    iota("i_g", A("iog", 0, 128), [[1, 8], [0, 16]], 0, 0)
    iota("i_w", A("iow", 0, 3 * RG), [[0, 3], [1, RG]], 0, 0)
    iota("i_k", A("keep", 0, 288), [[0, 36], [1, 8]], 0, 0)
    iota("i_e", A("ee", 0, 36), [[16, 36]], 257, 1)
    ts("c_g", col("ci", 1), col("ci", 0), 4, ALU.logical_shift_right)
    ts("c_zc", col("cf", 1), col("ci", 1), 16.0, ALU.mult, 15.0, ALU.add)
    same("c_z", A("zz", 0, 144), A("ioy", 0, 144), col("cf", 1))
    lin("c_z8", A("z8", 0, 144), A("zz", 0, 144), 8192.0, 0.0)
    lin("c_zf", A("zf", 0, 144), A("zz", 0, 144), 1.0 / W, 0.0)
    same("c_id", id1, A("ioy", 0, 128), col("cf", 0))
    lin("c_idn", idn, id1, -1.0, 0.0)
    lin("c_idk", A("idk", 0, 128), id1, 2048.0, 0.0)
    ts("c_i", col("ci", 4), col("ci", 0), 15, ALU.bitwise_and)
    cp("c_if", col("cf", 9), col("ci", 4))
    lin("c_j", A("jc", 0, 64), A("ioj", 0, 64), 1.0, col("cf", 9))
    ts("c_b", col("ci", 2), col("ci", 0), 3, ALU.bitwise_and)
    ts("c_a", col("ci", 3), col("ci", 0), 2, ALU.logical_shift_right, 3, ALU.bitwise_and)
    cp("c_af", col("cf", 3), col("ci", 3))
    ts("c_h", col("cf", 5), col("ci", 2), 16.0, ALU.mult, col("cf", 3), ALU.add)
    ts("c_l1", A("l1", 0, 9), A("iol", 0, 9), col("cf", 5), ALU.add)
    ts("c_l2", A("l2", 0, 3), A("iol", 0, 3), col("cf", 3), ALU.add)
    ts("c_m1", col("cf", 6), col("ci", 4), 1.0, ALU.is_equal)
    ts("c_m0", col("cf", 7), col("ci", 4), 0.0, ALU.is_equal, 2.0 * W, ALU.mult)
    lin("c_wi", A("wi", 0, 12), A("ioy", 0, 12), 16.0, col("cf", 9))
    cp("c_gf", col("cf", 8), col("ci", 1))
    same("c_blk", blk, A("iog", 0, 128), col("cf", 8))
    lin("c_gt0", A("gt0", 0, 128), blk, -1.0, 0.0)
    add("c_gtn", {"pool": 0.21 + 256 * CY},
        lambda q, T, e, R: q.affine_select(T.gtn[:], T.gt0[:], [[-1, 128]], ALU.is_gt, 0.0, 0, 1), [A("gt0", 0, 128)], [A("gtn", 0, 128)])
    lin("c_fb", A("fb", 2048, 2048 + 3 * RG), A("iow", 0, 3 * RG), col("cf", 6), col("cf", 7))
    lin("c_m128", A("m128", 0, RG), A("iow", 0, RG), 0.0, -128.0)
    cp("pinu", pu(0, 12, 76), X("pw", 0, ALL))
    cp("cuu", pu(0, 0, 12), A("cus", 0, 12))
    ts("th8", A("th8", 0, 64), A("ths", 0, 64), 8192.0, ALU.mult)
    send("st", [("th%d" % c, ("t", c), A("thn", 16 * c, 16 * c + 16), A("th8", 16 * c, 16 * c + 16)) for c in range(NCH)])
    ts("fr_t", A("frt", 0, RG), A("frs", 0, RG), col("cf", 6), ALU.mult)
    tt("fr_d", A("f0", 0, RG), A("frs", 0, RG), A("frt", 0, RG), ALU.subtract)
    for h, H in enumerate("AB"):
        lin("q" + H, A("qin", HF * h, HF * h + HF), A("qraw", HF * h, HF * h + HF), SCL[0], SCL[0] * QB[0])

    def release(p):
        K = p + 1
        n8, n1 = 96 * K, 12 * K
        tt("bit", A("bin", 64 * p, 64 * p + 64), A("kin", 64 * p, 64 * p + 64), A("thn", 0, 64), ALU.is_ge)
        gtt("mo", A("hm", 288 * K + 1, 288 * K + n8, 2), A("bin", 64 * p, 64 * p + 64), A("l1", 0, 3 * K),
            A("hm", 288 * p, 288 * p + n8, 2), ALU.mult)
        scan("ho", A("ho", 0, n8), A("keep", 0, n8), A("hm", 288 * K, 288 * K + n8), ALU.mult, ALU.max)
        rel, cum = A("rel", 0, n1), A("cum", 0, n1)
        if p:
            tt("rel", rel, A("valid", 0, n1), A("ho", 7, n8, 8), ALU.is_gt)
        else:
            ts("rel", rel, A("ho", 7, n8, 8), 0.5, ALU.is_lt)
        scan("cum", cum, rel, rel, ALU.add, ALU.max)
        mm("rk", [(A("ws", 0, n1), A("gtn", 0, 128), rel), (A("ws", 0, n1), A("idk", 0, 128), rel),
                  (A("ws", 0, n1), blk, cum), (A("ws", 40, 41), blk, A("cum", n1 - 1, n1))])
        tt("pos", A("pos", 0, n1), A("ws", 0, n1), A("ee", 0, n1), ALU.max)
        ts("posu", A("posu", 0, n1), A("pos", 0, n1), -1.0, ALU.add)
        if p == 0:
            lin("vv", A("valid", 0, n1), rel, -1.0, 1.0)
        elif p < PH - 2:
            tt("vv", A("valid", 0, n1), A("valid", 0, n1), rel, ALU.subtract)
        va = A("valid", n1, n1 + 12)
        ts("ac", va, A("wi", 0, 12), A("ws", 40, 41), ALU.is_lt)
        tt("ad", A("mx", 0, 12), A("a4", 16 * K, 16 * K + 12), va, ALU.subtract)
        ts("au", A("au", 16 * K, 16 * K + 12), A("mx", 0, 12), float(W), ALU.mult)
        for k in range(K):
            scatter("sl%d" % k, A("fb", RG * p, RG * p + 2048 + RG), A("posu", 12 * k, 12 * k + 12),
                    A("g0", 1216 * k, 1216 * k + RG))

    for p in range(PH):
        now[0] = p
        last = p == PH - 1
        free = A("f0", 0, RG) if p == 0 else A("fb", 2048 + RG * (p - 1), 2048 + RG * p)
        s, G, r0 = SCL[p], 1216 * p, A("wr", 0, RG)
        fu, au, a4 = A("fu", 16 * p, 16 * p + 12), A("au", 16 * p, 16 * p + 12), A("a4", 16 * p, 16 * p + 12)
        if p == 0:
            au = pu(0, 0, 12)
        XH = [2 * HF * (h + 2 * (p % 2)) for h in range(2)]
        g1, G1 = ("g0", 1216) if p == 0 else ("g1", 0)
        n2, N2 = ("n1u", 80) if p == 0 else ("n2u", 80 * p)
        for h, H in enumerate("AB"):
            bank, k0, k1 = ("wa", 0, 44) if h == 0 else ("wb", 44, 76)
            ka, kb = max(k0, 12) if p == 1 else k0, max(k0, 12) if p else k0
            gather("g0" + H, A("g0", G + 16 * ka, G + 16 * k1), mw, pu(2 * p, ka, k1))
            wrap("w0" + H, bank, "zz", "g0", G + 16 * ka, G + 16 * k1)
            cp("nu0" + H, A("n1u", 80 * p + ka, 80 * p + k1), A(bank, 0, k1 - ka))
            lin("nk0" + H, nk(p, 0, ka, k1), A(bank, 0, k1 - ka), 1.0, 0.0)
            gather("g1" + H, A(g1, G1 + 16 * k0, G1 + 16 * k1), mw, A("n1u", 80 * p + k0, 80 * p + k1))
            wrap("w1" + H, bank, "zz", g1, G1 + 16 * kb, G1 + 16 * k1)
            cp("nu1" + H, A(n2, N2 + kb, N2 + k1), A(bank, 0, k1 - kb))
            lin("nk1" + H, nk(p, 1, kb, k1), A(bank, 0, k1 - kb), 1.0, float(W))
            gather("x1" + H, A("xh", XH[h], XH[h] + HF), xw, A("n1u", 80 * p + k1 - 32, 80 * p + k1), s, s * (TB[p] - 0.5))
            gather("x2" + H, A("xh", XH[h] + HF, XH[h] + 2 * HF), xw, A(n2, N2 + k1 - 32, N2 + k1), s, s * (TB[p] - 0.5))
        if not last:
            if p != 1:
                gather("xa", A("xab", 0, RG), xw, pu(2 * p, 0, 12))
            gather("xb", A("xab", RG, 2 * RG), xw, A("n1u", 80 * p, 80 * p + 12))
            mm("xs", [(r0, id1, A("xv" if p == 1 else "xab", 0, RG)), (r0, id1, A("xab", RG, 2 * RG))])
            lin("xv", A("xv", 0, RG), r0, 0.5, 63.75 if p == 1 else 127.75)
        else:
            o = A("wr", 0, 256)
            mm("wn", [(o, A("zz", 15 - i, 143 - i), A("mt", 256 * i, 256 * i + 256)) for i in range(16)])
            lin("ynf", A("ynf", 0, 256), o, 1.0, 0.0)
            move("mf", "sp", rows("mf", 0, W), A("ynf", 0, 256))
            mm("nbs", [(r0, blk, A("g1", 0, RG))])
            lin("nbf", A("ff", RG, 2 * RG), r0, 1.0, 0.0)
        if p:
            release(p - 1)
        fw = A("ws", 0, 12)
        wrap("wf", "ws", "zf", free[0], free[2][0][0], free[2][0][1])
        ts("fu", fu, fw, float(W), ALU.mult)
        if not last:
            a4n = A("a4", 16 * p + 16, 16 * p + 28)
            if p:
                tt("mn", A("mn", 0, 12), fw, a4, ALU.min)
                tt("a4", a4n, A("mn", 0, 12), A("valid", 12 * p, 12 * p + 12), ALU.add)
                ts("anu", pu(2 * p + 2, 0, 12), a4n, -1.0, ALU.add, float(W), ALU.mult)
            else:
                lin("a4", a4n, fw, 1.0, 1.0)
            scatter("sa", A("mt", 0, TW), au, free)
            scatter("sf", A("mt", 0, TW), fu, A(g1, G1, G1 + RG))
            scatter("sx", A("xt", 0, TW), fu, A("xv", 0, RG), A("m128", 0, RG))
        else:
            mm("fs", [(r0, blk, free)])
            lin("ff", A("ff", 0, RG), r0, 1.0, 0.0)
            scatter("sf", A("mf", 0, TW), fu, A("ff", RG, 2 * RG))
            scatter("sa", A("mf", 0, TW), au, A("ff", 0, RG))
        for h, H in enumerate("AB"):
            b, bank = XH[h], "wa" if h == 0 else "wb"
            for u in range(2):
                d, c = "d%d" % (2 * h + u), 2 * h + u
                if MODE[p] == "hop":
                    nm, ab = "%d%s" % (u + 1, H), X("ab", u, slice(HF * h, HF * h + HF))
                    mm("dq" + nm, [(A(d, 0, HF), idn, A("qin", 1024 * p + HF * h, 1024 * p + HF * h + HF))], (p, d))
                    mm("dx" + nm, [(A(d, 0, HF), id1, A("xh", b + HF * u, b + HF * u + HF))], (p, d))
                else:
                    nm, ab = "%d" % c, X("ab", ALL, slice(CH * c, CH * c + CH))
                    qa = A("qin", 1024 * p + CH * c, 1024 * p + CH * c + CH)
                    for hop in range(2):
                        xc = b + HF * hop + CH * u
                        mm("dx%d%d" % (hop + 1, c), [(A(d, CH * hop, CH * hop + CH), id1, A("xh", xc, xc + CH))], (p, d))
                    mm("dq" + nm, [(A(d, 0, CH), idn, qa), (A(d, CH, 2 * CH), idn, qa)], (p, d))
                add("ab" + nm, {"act": cyc(HF)},
                    lambda q, T, e, R, ab=ab, d=d, p=p: q.activation(ap(T, ab), T[d][:, 0:HF], AF.Abs, scale=1.0 / SCL[p],
                                                                     bias=QB[p] - TB[p] + 0.5), [A(d, 0, HF)], [ab])
            ks = slice(32 * h, 32 * h + 32)
            mm("wd" + H, [(A(bank, 0, 64), A("z8", 15 - i, 143 - i), X("ab", ALL, slice(HF * h + i, HF * h + HF, 16))) for i in range(16)])
            tt("ka" + H, X("key", 2 * h, ALL, ALL), A(bank, 0, 64), X("nk", p, ALL, slice(32 * h + 12, 32 * h + 44)), ALU.add)
            tt("kb" + H, X("key", 2 * h + 1, ALL, ALL), A(bank, 0, 64), A("jc", 0, 64), ALU.add)
            km = X("km", slice(2 * p, 2 * p + 2), ks)
            tt("min" + H, km, X("key", slice(2 * h, 2 * h + 2), 0, ALL), X("key", slice(2 * h, 2 * h + 2), 1, ALL), ALU.min)
            pw = X("pw", slice(2 * p + 2, 2 * p + 4), ks)
            ts("and" + H, pw, km, W - 1, ALU.bitwise_and)
            cp("pu" + H, X("pu", slice(2 * p + 2, 2 * p + 4), slice(32 * h + 12, 32 * h + 44)), pw)
            if h == 1 and not last:
                send("sb", [("b%d" % p, "b", A("kin", 64 * p, 64 * p + 64), X("km", 2 * p, ALL))])
            step = LAST[h] if last else 2
            for c in range(2 * h, 2 * h + 2, step):
                q0, q1 = 1024 * p + CH * c, 1024 * p + CH * (c + step)
                out = A("ss", CH * c, CH * (c + step)) if last else A("qout", q0, q1)
                if last and h == 0 and SPLIT[0]:
                    o = A("d%d" % c, 0, CH * step)
                    gather("sg%d" % c, out, A("xh", b, b + 2 * HF), pu(2 * p + 3, 12 + 16 * c, 12 + 16 * (c + step)))
                    mm("sm%d" % c, [(o, id1, A("qin", q0, q1)), (o, id1, out)])
                    ts("fin%d" % c, A("qout", q0, q1), o, RND, ALU.add, RND + 1.0, ALU.subtract)
                    store("yq%d" % c, "sp", lambda T, c=c, step=step: T.yq[:, CH * c:CH * (c + step)], A("qout", q0, q1))
                    continue
                gtt("sg%d" % c, out, A("xh", b, b + 2 * HF), pu(2 * p + 3, 12 + 16 * c, 12 + 16 * (c + step)), A("qin", q0, q1), ALU.add)
                if last:
                    ts("fin%d" % c, A("qout", q0, q1), out, RND, ALU.add, RND + 1.0, ALU.subtract)
                    store("yq%d" % c, "sp", lambda T, c=c, step=step: T.yq[:, CH * c:CH * (c + step)], A("qout", q0, q1))
                else:
                    send("sq" + H, [("q%d_%d" % (p, c + u), c + u, A("qin", q0 + 1024 + CH * u, q0 + 1024 + CH * u + CH),
                                     A("qout", q0 + CH * u, q0 + CH * u + CH)) for u in range(2)])
        if last:
            break
        K = p + 1
        if p == 1:
            gather("rx", A("retx", 48, 96), nk(0, 1, 0, 12), A("l2", 0, 3), 1.0, -float(W))
        else:
            gather("rx", A("retx", 48 * p, 48 * K), nk(p, 0, 0, 12), A("l2", 0, 3))
        gtt("eqo", A("hm", 384 * p, 384 * p + 96, 2), X("pw", 2 * p, ALL), A("l1", 0, 3), A("retx", 48 * p, 48 * K), ALU.is_equal)
        gtt("eqn", A("hm", 288 * K, 384 * K, 2), X("pw", 2 * p + 2, ALL), A("l1", 0, 3 * K), A("retx", 0, 48 * K), ALU.is_equal)
    cp("ypf", A("ypf", 0, 64), X("pw", 8, ALL))
    store("yp", "sp", lambda T: T.yp[:], A("ypf", 0, 64))
    store("yn", "sp", lambda T: T.yn[:], rows("mf", 0, W))
    return ops


def meet(a, b):
    if a[0] != b[0]:
        return False
    if SCRATCH[a[0]][0] == "psum":
        return True
    return bool(a[3] & b[3]) and any(x0 < y1 and y0 < x1 for x0, x1 in a[2] for y0, y1 in b[2])


def find_deps(ops):
    deps = []
    for k, o in enumerate(ops):
        d = {}
        mine = {a[0] for a in o["r"] + o["w"]}
        for j in range(k):
            e = ops[j]
            if not any(b[0] in mine for b in e["r"] + e["w"]) or o.get("group") and o["group"] == e.get("group"):
                continue
            if any(meet(a, b) for a in o["r"] + o["w"] for b in e["w"]) or any(meet(a, b) for a in o["w"] for b in e["r"]):
                d[j] = False
            elif any(SCRATCH[a[0]][0] == "psum" and meet(a, b) for a in o["r"] for b in e["r"]):
                d[j] = True
        if o["after"] is not None:
            d[o["after"]] = False
        deps.append(d)
    return deps


QUEUES = {
    "sp": """
        l_nx l_q l_th l_fr1 l_fr0 l_cu l_pin l_hi l_lo l_x0 l_x1 l_mf.3 l_yn.3 l_yp.3 l_yq3.3 l_yq0.3 l_yq2.3""",
    "pool": """
        i_p i_y i_pf i_l i_j i_w i_e i_g st i_k sb.0 sqA.0 sqB.0 c_gtn sb.1 sqA.1 sqB.1 sb.2 sqA.2 sqB.2""",
    "pe": """
        wf.0 w0B.0 w0A.0 dq2B.0 dq1B.0 w1B.0 w1A.0 dx1B.0 dq1A.0 dx2B.0 dq2A.0 dx1A.0 dx2A.0 wdB.0 wdA.0 xs.0 w0A.1 w0B.1 w1A.1
        dx1B.1 w1B.1 rk.1 dx1A.1 dx2A.1 dq1A.1 dq2A.1 wf.1 dq1B.1 dq2B.1 dx2B.1 wdA.1 wdB.1 xs.1 w0A.2 w0B.2 w1A.2 w1B.2 dx1A.2
        rk.2 dx1B.2 xs.2 dq1A.2 dx2A.2 dq2A.2 dx2B.2 dq2B.2 dq1B.2 wf.2 wdA.2 wdB.2 wn.3 w0A.3 w0B.3 w1A.3 nbs.3 w1B.3 rk.3
        dx1A.3 dx1B.3 dx2A.3 dq2A.3 dq1A.3 dx2B.3 dq1B.3 dq2B.3 wdA.3 wf.3 fs.3 wdB.3 sm0.3""",
    "act": """
        z5 z6 z3 qB c_za c_z c_ida c_zf c_id g0B.0 qA g1B.0 nk0B.0 rx.0 x1B.0 x1A.0 ab1B.0 ab2B.0 ab1A.0 ab2A.0 xa.0 xb.0
        c_blka c_blk xv.0 g0A.1 g0B.1 g1A.1 g1B.1 x1A.1 x2A.1 x2B.1 ab1A.1 ab2A.1 ab1B.1 ab2B.1 xb.1 g0A.2 xv.1 vv.1 g0B.2
        g1A.2 x1A.2 x1B.2 x2A.2 x2B.2 ab1A.2 ab2A.2 ab2B.2 ab1B.2 xv.2 rx.2 g0A.3 g0B.3 g1A.3 x1A.3 x1B.3 x2A.3 x2B.3 ab2A.3
        ab1A.3 ab1B.3 ab2B.3 ff.3 sg0.3""",
    "dve": """
        z0 zfr z7 z1 z4 hi lo c_g th8 c_zc c_i c_a c_gf c_m1 pinu c_af c_m128 c_b c_l2 fr_t cuu fr_d c_idn g0A.0 c_z8 nu0B.0
        c_h c_if fu.0 c_wi nu0A.0 nk0A.0 g1A.0 c_m0 nu1B.0 c_j x2B.0 nu1A.0 nk1B.0 c_l1 x2A.0 sa.0 nk1A.0 sf.0 kaB.0 kbB.0
        kaA.0 kbA.0 minB.0 minA.0 andA.0 andB.0 puA.0 puB.0 sg0.0 sg2.0 nu0A.1 sx.0 nu0B.1 nk0A.1 eqo.0 x1B.1 c_idk a4.0 eqn.0
        nk0B.1 bit.1 c_gt0 nu1A.1 mo.1 rx.1 ho.1 rel.1 nu1B.1 cum.1 c_fb nk1B.1 pos.1 ac.1 posu.1 ad.1 sl0.1 au.1 sa.1 nk1A.1
        fu.1 eqo.1 sf.1 kaA.1 kbA.1 mn.1 minA.1 a4.1 andA.1 anu.1 puA.1 kaB.1 kbB.1 minB.1 sg0.1 andB.1 puB.1 sg2.1 nu0A.2
        eqn.1 sx.1 nu0B.2 nk0B.2 nk0A.2 g1B.2 xa.2 bit.2 nu1A.2 mo.2 nu1B.2 ho.2 nk1A.2 rel.2 cum.2 xb.2 pos.2 ac.2 posu.2 ad.2
        sl0.2 au.2 sl1.2 nk1B.2 sa.2 fu.2 mn.2 sf.2 kaA.2 kbA.2 kaB.2 kbB.2 minA.2 minB.2 a4.2 andA.2 anu.2 puA.2 andB.2 sg0.2
        puB.2 eqo.2 sg2.2 nu0A.3 nk0A.3 sx.2 nu0B.3 vv.2 ynf.3 eqn.2 g1B.3 bit.3 nk0B.3 mo.3 nu1A.3 ho.3 rel.3 cum.3 nu1B.3
        nbf.3 pos.3 ac.3 posu.3 nk1A.3 sl0.3 sl1.3 ad.3 sl2.3 au.3 kaA.3 kbA.3 minA.3 nk1B.3 andA.3 fu.3 puA.3 sf.3 kaB.3 kbB.3
        sa.3 minB.3 andB.3 puB.3 ypf.3 sg3.3 fin3.3 fin0.3 sg2.3 fin2.3""",
}


def plan():
    ops = build_ops()
    deps = find_deps(ops)
    number = {o["name"] + ("" if o["p"] == "" else ".%d" % o["p"]): k for k, o in enumerate(ops)}
    lists = {e: [number[w] for w in text.split()] for e, text in QUEUES.items()}
    eng, order, done = [None] * len(ops), [], set()
    while len(order) < len(ops):
        before = len(order)
        for e, calls in lists.items():
            while calls and all(j in done for j in deps[calls[0]]):
                k = calls.pop(0)
                eng[k] = e
                new = [k, k + 1] if ops[k]["kind"] == "send" else [k]
                order += new
                done.update(new)
        assert len(order) > before
    for k in order:
        if ops[k].get("group"):
            mates = [j for j in order if ops[j].get("group") == ops[k]["group"]]
            ops[k].update({"first": k == mates[0], "last": k == mates[-1]})
    return ops, deps, eng, order


PLAN = []


def ways(T, topo, r):
    src, nxt, prv = T.cores[r], T.cores[(r + 1) % len(T.cores)], T.cores[r - 1]
    able = [c for c in topo.cores_of(src) if T.rank_of(c) is None and topo.may_write(c, nxt) and topo.may_write(c, prv)]
    near = [c for c in able if topo.die(c) == topo.die(src)]
    far = [c for c in able if c not in near]
    lane = [c for pair in zip(near, far) for c in pair]
    out = {"b": [src, prv] if topo.may_write(src, prv) else [src, lane[2], prv]}
    for c in range(NCH):
        out[c] = [src, nxt] if lane[c] in near and topo.may_write(src, nxt) else [src, lane[c], nxt]
        out["t", c] = [src, lane[c], prv]
    return out


def shares(topo, paths):
    allowed = [topo.engines(w[0], w[1]) for w in paths]
    most, taken, out = max(len(a) for a in allowed) // len(paths), [], {}
    for k in sorted(range(len(paths)), key=lambda k: len(allowed[k])):
        out[k] = [e for e in allowed[k] if e not in taken][:most]
        taken += out[k]
    return [out[k] for k in range(len(paths))]


def relay_program(g, core, T, topo, ops, order):
    sent = 0
    for r in [r for r, c in enumerate(T.cores) if core in topo.cores_of(c)]:
        way = ways(T, topo, r)
        for k in order:
            if ops[k]["kind"] != "recv":
                continue
            paths = [way[x[1]] for x in ops[k]["emit"]]
            for (sem, name, place, source), path, used in zip(ops[k]["emit"], paths, shares(topo, paths)):
                if len(path) == 3 and path[1] == core:
                    piece = T[place[0]][place[1]]
                    rid, pid = topo.addr(path[2], core)
                    g.wait_ge(T.sem[sem], len(used))
                    g.remote_dma(piece, piece, T.sem[sem], T.sem.sent, pid, rid, topo.mask(core, path[2]))
                    sent += len(topo.engines(core, path[2]))
    if sent:
        g.wait_ge(T.sem.sent, sent)


def rank_program(g, core, T, topo):
    if not PLAN:
        PLAN.append(plan())
    ops, deps, eng, order = PLAN[0]
    rank = T.rank_of(core)
    if rank is None:
        relay_program(g, core, T, topo, ops, order)
        return
    n = len(T.cores)
    out = ways(T, topo, rank)

    def R(names):
        paths = [out[s] for s in names]
        return [topo.addr(w[1], core) + (sum(1 << e for e in used),) for w, used in zip(paths, shares(topo, paths))]
    comes = dict(ways(T, topo, (rank - 1) % n))
    comes.update({s: w for s, w in ways(T, topo, (rank + 1) % n).items() if s not in range(NCH)})
    token, total, sent = {}, {}, 0
    for k in order:
        o = ops[k]
        if o["kind"] == "c":
            total[eng[k]] = total.get(eng[k], 0) + 1
            token[k] = [(eng[k], total[eng[k]])]
        elif o["kind"] == "dma":
            token[k] = [(o["sem"], 16)]
        elif o["kind"] == "recv":
            paths = [comes[x[1]] for x in o["emit"]]
            token[k] = [(x[0], len(used if len(w) == 2 else topo.engines(w[1], core)))
                        for x, w, used in zip(o["emit"], paths, shares(topo, paths))]
            sent += sum(len(used) for used in shares(topo, [out[x[1]] for x in o["emit"]]))
    queue = {"dve": g.vector, "act": g.scalar, "pe": g.tensor, "pool": g, "sp": g.sync}
    waited, seen = {}, {e: {} for e in queue}
    for k in order:
        e = eng[k]
        if e is None:
            continue
        need = {}
        for j, both_read in deps[k].items():
            if not (eng[j] == e and (e == "pe" or both_read)):
                for s, v in token[j]:
                    need[s] = max(need.get(s, 0), v)
        for s, v in need.items():
            if seen[e].get(s, 0) < v:
                queue[e].wait_ge(T.sem[s], v)
                seen[e][s] = v
                waited[s] = max(waited.get(s, 0), v)
        ins = ops[k]["emit"](queue[e], T, e, R)
        if ops[k]["kind"] != "send":
            ins.then_inc(T.sem[token[k][0][0]], 1 if ops[k]["kind"] == "c" else 16)
    g.wait_ge(T.sem.sent, sent)
    for s, v in list(total.items()) + [t for k in token for t in token[k] if ops[k]["kind"] != "c"]:
        if waited.get(s, 0) < v:
            g.sync.wait_ge(T.sem[s], v)
